import numpy as np
import ml_dtypes


def mxq(x, axis, fmt="e4m3"):
    dtype, down = {"e4m3": (ml_dtypes.float8_e4m3fn, 7), "e5m2": (ml_dtypes.float8_e5m2, 14)}[fmt]
    v = np.moveaxis(np.asarray(x, np.float32).astype(ml_dtypes.bfloat16).astype(np.float64), axis, -1)
    blocks = v.reshape(v.shape[:-1] + (-1, 32))
    amax = np.abs(blocks).max(-1, keepdims=True)
    byte = np.maximum(np.where(amax > 0, np.frexp(amax)[1] - 1 + 127, 0) - down, 1)
    scale = np.exp2(byte - 127.0)
    codes = (blocks / scale).astype(np.float32).astype(dtype).astype(np.float64)
    return np.moveaxis((codes * scale).reshape(v.shape), -1, axis)


WIDE = False


def mx_kscale(k):
    if not WIDE:
        return np.ones(k)
    levels = np.array([10, -10, 5, -5, 0])
    if k % 512:
        return np.exp2(np.random.permutation(np.resize(levels, k // 32))).repeat(32)
    a = np.empty((k // 512, 16))
    for p in range(k // 512):
        a[p, :8] = np.random.permutation(np.resize(levels, 8))
        for g in range(8):
            far = levels[np.abs(levels - a[p, g]) >= 10]
            a[p, g + 8] = far[np.random.randint(len(far))]
    return np.exp2(a.ravel()).repeat(32)


def f64(x):
    return np.asarray(x).astype(np.float64)


def striped(idx):
    return np.tile(idx.reshape(-1, 16).T, (8, 1)).astype(np.uint16)


def unstriped(offs):
    return offs[:16].T.reshape(-1).astype(np.int64)


E2M1 = np.array([0.0, 0.5, 1.0, 1.5, 2.0, 3.0, 4.0, 6.0, -0.0, -0.5, -1.0, -1.5, -2.0, -3.0, -4.0, -6.0])


def pack_weight(w, fmt):
    k, n = w.shape
    w = f64(np.asarray(w, np.float32).astype(ml_dtypes.bfloat16)).reshape(k // 32, 32, n)
    amax = np.abs(w).max(1)
    if fmt == "e4m3":
        byte = np.frexp(amax)[1] - 1 + 127 - 7
    else:
        mant, ex = np.frexp(amax / 6.0)
        byte = np.where(mant > 0.5, ex, ex - 1) + 127
    byte = np.clip(np.where(amax > 0, byte, 1), 1, 254)
    scaled = (w * np.exp2(127.0 - byte)[:, None, :]).reshape(k, n).astype(np.float32)
    by_word = np.ascontiguousarray(scaled.reshape(k // 512, 128, 4, n).transpose(0, 1, 3, 2))
    if fmt == "e4m3":
        words = by_word.astype(ml_dtypes.float8_e4m3fn).view(np.uint8)
    else:
        c = by_word.astype(ml_dtypes.float4_e2m1fn).view(np.uint8) & 0xF
        words = (c[..., 0::2] | (c[..., 1::2] << 4)).reshape(k // 512, 128, 2 * n)
    return np.ascontiguousarray(words), np.ascontiguousarray(byte.astype(np.uint8).reshape(k // 512, 16, n))


def unpack_weight(words, scales, fmt):
    g, _, n = scales.shape
    words = np.ascontiguousarray(words).reshape(g, 128, n, -1)
    if fmt == "e4m3":
        vals = words.view(ml_dtypes.float8_e4m3fn).astype(np.float64)
    else:
        nib = np.empty((g, 128, n, 4), np.uint8)
        nib[..., 0::2] = words & 0xF
        nib[..., 1::2] = words >> 4
        vals = E2M1[nib]
    vals = vals * np.repeat(np.exp2(scales.astype(np.float64) - 127.0), 8, axis=1)[..., None]
    return vals.transpose(0, 1, 3, 2).reshape(g * 512, n)


def gelu(v):
    return 0.5 * v * (1.0 + np.tanh(np.sqrt(2.0 / np.pi) * (v + 0.044715 * v**3)))


K, H, T, S, T3, S2, T2 = 1024, 1024, 2048, 512, 1024, 512, 1024

def setup_inputs():
    n = np.random.standard_normal
    s = mx_kscale(K)[:, None]
    u = s
    tab_words, tab_scales = pack_weight(n((K, T)) * s, "e4m3")
    tab2_words, tab2_scales = pack_weight(n((H, T3)) / np.sqrt(H) / u, "e4m3")
    w2_words, w2_scales = pack_weight(0.8 * n((K, H)) / np.sqrt(K) / s * u.T, "e2m1")
    return {
        "tab_words": tab_words, "tab_scales": tab_scales,
        "tab2_words": tab2_words, "tab2_scales": tab2_scales,
        "offs": striped(np.random.permutation(T)[:S]),
        "offs2": striped(np.random.permutation(T3)[:S2]),
        "offs3": striped(np.random.permutation(T2)[:S]),
        "w1": (n((K, H)) / np.sqrt(K) / s).astype(np.float32),
        "w2_words": w2_words, "w2_scales": w2_scales,
        "season": (1.3 * np.exp(0.4 * n((H, S)))).astype(np.float32),
        "gain": (1.2 * np.exp(0.3 * n(H)) * u[:, 0]).astype(np.float32),
        "ex": np.exp(0.4 * n(S2)).astype(np.float32),
        "page1": (0.7 * n((S2, T2))).astype(np.float32),
        "wgo": np.exp(0.3 * n((128, S))).astype(np.float32),
    }

def reference(tab_words, tab_scales, tab2_words, tab2_scales, offs, offs2, offs3, w1, w2_words, w2_scales, season, gain, ex, page1, wgo):
    v = unpack_weight(tab_words, tab_scales, "e4m3")[:, unstriped(offs)]
    v2 = unpack_weight(tab2_words, tab2_scales, "e4m3")[:, unstriped(offs2)]
    b1 = mxq(f64(w1), 0, "e4m3").T @ v
    b2 = unpack_weight(w2_words, w2_scales, "e2m1").T @ v
    h = f64(gain)[:, None] * np.tanh(f64(season) * b1) + b2
    e = v2.T @ mxq(h, 0, "e4m3")
    d = v2.T @ v
    y = np.tanh(f64(ex)[:, None] * e + d)
    out = f64(page1).copy()
    out[:, unstriped(offs3)] = np.tile(f64(wgo), (S2 // 128, 1)) * y
    return out

@@ -1,0 +1,238 @@
+from contextlib import ExitStack
+
+import concourse.mybir as mybir
+
+K, H, T, S, T3, S2, T2 = 1024, 1024, 2048, 512, 1024, 512, 1024
+FLOPS = 2 * S * (2 * K * H + S2 * H + S2 * K)
+
+F32 = mybir.dt.float32
+BF16 = mybir.dt.bfloat16
+I32 = mybir.dt.int32
+U32 = mybir.dt.uint32
+U16 = mybir.dt.uint16
+U8 = mybir.dt.uint8
+FP8X4 = mybir.dt.float8_e4m3fn_x4
+FP4X4 = mybir.dt.float4_e2m1fn_x4
+MULT = mybir.AluOpType.mult
+ADD = mybir.AluOpType.add
+TANH = mybir.ActivationFunctionType.Tanh
+
+P = 128
+PACK = 4
+KP = P * PACK
+PASSES = 2
+JH = S // 2
+SCALAR_SHARE = {(0, 0): 128, (1, 0): 40, (0, 1): 128, (1, 1): 40}
+
+
+def tile_list_star_conference_scores_kernel(
+    tc, tab_words, tab_scales, tab2_words, tab2_scales, offs, offs2, offs3,
+    w1, w2_words, w2_scales, season, gain, ex, page1, wgo, out,
+):
+    nc = tc.nc
+    with ExitStack() as ctx:
+        held = ctx.enter_context(tc.tile_pool(name="held", bufs=1))
+        ring = ctx.enter_context(tc.tile_pool(name="ring", bufs=3))
+        stage = ctx.enter_context(tc.tile_pool(name="stage", bufs=4))
+        psum = ctx.enter_context(tc.psum_pool(name="psum", bufs=4))
+
+        def keep(shape, dtype, name):
+            return held.tile(shape, dtype, name=name, align_bytes=64)
+
+        def staged(shape, dtype, name):
+            return stage.tile(shape, dtype, name=name, tag="staged", align_bytes=64)
+
+        lst = keep([P, S // 16], U16, "lst")
+        lst2 = keep([P, S2 // 16], U16, "lst2")
+        lst3 = keep([P, S // 16], U16, "lst3")
+
+        def load_scales(dram, plane):
+            nc.gpsimd.memset(plane[:].bitcast(I32), 0)
+            for q in range(4):
+                nc.scalar.dma_start(
+                    out=plane[32 * q : 32 * q + 8, :].bitcast(I32),
+                    in_=dram[:, 4 * q : 4 * q + 4, :].bitcast(I32),
+                )
+
+        nc.sync.dma_start(lst[:], offs)
+        nc.sync.dma_start(lst2[:], offs2)
+        nc.sync.dma_start(lst3[:], offs3)
+        tabw = [staged([P, T], U32, "tabw%d" % a) for a in range(PASSES)]
+        for a in range(PASSES):
+            nc.sync.dma_start(
+                out=tabw[a][:].bitcast(I32), in_=tab_words[a].rearrange("p t i -> p (t i)").bitcast(I32)
+            )
+        tabs = staged([P, T], U8, "tabs")
+        load_scales(tab_scales, tabs)
+        tab2s = staged([P, T3], U8, "tab2s")
+        load_scales(tab2_scales, tab2s)
+        w2s_raw = held.tile([P, PASSES * H], U8, name="w2s_raw", tag="w2s_raw", align_bytes=64)
+        nc.gpsimd.memset(w2s_raw[:].bitcast(I32), 0)
+        for q in range(4):
+            nc.scalar.dma_start(
+                out=w2s_raw[32 * q : 32 * q + 4, :].bitcast(I32).rearrange("r (a c) -> r a c", a=PASSES),
+                in_=w2_scales[:, 4 * q : 4 * q + 4, :].bitcast(I32).rearrange("a r c -> r a c"),
+            )
+
+        vs = keep([P, S], U8, "vs")
+        nc.vector.tensor_copy(vs[:], tabs[:].indirect(lst[:]))
+        vs1 = keep([P, S], U8, "vs1")
+        nc.gpsimd.memset(vs1[:].bitcast(I32), 0)
+        nc.scalar.dma_start(out=vs1[0:112, :].bitcast(I32), in_=vs[4:116, :].bitcast(I32))
+        vs_low = [vs, vs1]
+        vw = [keep([P, S], U32, "vw%d" % a) for a in range(PASSES)]
+        v2w = [keep([P, S2], U32, "v2w%d" % a) for a in range(PASSES)]
+        v2s = keep([P, S2], U8, "v2s")
+        for a in range(PASSES):
+            nc.vector.tensor_copy(vw[a][:], tabw[a][:].indirect(lst[:]))
+        nc.vector.tensor_copy(v2s[:], tab2s[:].indirect(lst2[:]))
+
+        tab2w = staged([P, PASSES * T3], U32, "tab2w")
+        nc.sync.dma_start(
+            out=tab2w[:].bitcast(I32).rearrange("p (a c) -> p a c", a=PASSES),
+            in_=tab2_words.rearrange("a p t i -> p a (t i)").bitcast(I32),
+        )
+        w2_raw = staged([P, PASSES * H], U16, "w2_raw")
+        nc.sync.dma_start(
+            out=w2_raw[:].bitcast(I32).rearrange("p (a c) -> p a c", a=PASSES),
+            in_=w2_words.rearrange("a p c -> p a c").bitcast(I32),
+        )
+        for a in range(PASSES):
+            nc.vector.tensor_copy(v2w[a][:], tab2w[:, T3 * a : T3 * (a + 1)].indirect(lst2[:]))
+        w2s = keep([P, PASSES * H], U8, "w2s")
+        nc.vector.tensor_copy(
+            out=w2s[:].rearrange("p (g t m) -> p g t m", t=PACK, m=P),
+            in_=w2s_raw[:].rearrange("p (g m t) -> p g t m", t=PACK, m=P),
+        )
+
+        factors = held.tile([P, 16], F32, name="factors", tag="w2s_raw", align_bytes=64)
+        gain_sb = factors[:, 0:8].rearrange("p (b t) -> p b t", b=PASSES)
+        ex_sb = factors[:, 8:12]
+        nc.sync.dma_start(out=gain_sb, in_=gain.rearrange("(b p t) -> p b t", b=PASSES, t=PACK))
+        with nc.allow_non_contiguous_dma(reason="one value a partition"):
+            nc.sync.dma_start(out=ex_sb, in_=ex.rearrange("(c p) -> p c", p=P))
+
+        d_sb = []
+        for c in range(S2 // P):
+            cols = slice(P * c, P * (c + 1))
+            acc = psum.tile([P, S], F32, name="acc2")
+            for a in range(PASSES):
+                nc.tensor.matmul_mx(
+                    out=acc[:], lhsT=v2w[a][:, cols].bitcast(FP8X4), lhsT_scale=v2s[4 * a :, cols],
+                    rhs=vw[a][:].bitcast(FP8X4), rhs_scale=vs[4 * a :, :], start=(a == 0), stop=(a == PASSES - 1),
+                )
+            d_sb.append(keep([P, S], F32, "d_sb%d" % c))
+            nc.scalar.copy(out=d_sb[c][:], in_=acc[:])
+
+        w2w = keep([P, PASSES * H], U16, "w2w")
+        nc.vector.tensor_copy(
+            out=w2w[:].rearrange("p (g t m) -> p g t m", t=PACK, m=P),
+            in_=w2_raw[:].rearrange("p (g m t) -> p g t m", t=PACK, m=P),
+        )
+
+        h_words = {}
+        h_scales = {}
+        for b in range(PASSES):
+            w1w, w1s = [], []
+            for a in range(PASSES):
+                w1_raw = staged([P, PACK, KP], F32, "w1_raw")
+                nc.sync.dma_start(
+                    out=w1_raw[:],
+                    in_=w1[KP * a : KP * (a + 1), KP * b : KP * (b + 1)].rearrange("(p j) c -> p j c", j=PACK),
+                )
+                grouped = ring.tile([P, PACK, P, PACK], BF16, name="grouped", tag="grouped", bufs=2, align_bytes=64)
+                dst = grouped[:].rearrange("p t m j -> p m j t")
+                src = w1_raw[:].rearrange("p j (m t) -> p m j t", t=PACK)
+                cut = SCALAR_SHARE[a, b]
+                nc.scalar.copy(out=dst[:, :cut], in_=src[:, :cut])
+                if cut < P:
+                    nc.vector.tensor_copy(out=dst[:, cut:], in_=src[:, cut:])
+                w1w.append(keep([P, KP], U32, "w1w%d%d" % (a, b)))
+                w1s.append(keep([P, KP], U8, "w1s%d%d" % (a, b)))
+                nc.vector.quantize_mx(
+                    out=w1w[a][:].bitcast(FP8X4), scales=w1s[a][:],
+                    in_=grouped[:].rearrange("p t m j -> p (t m j)"),
+                )
+            rows = season[KP * b : KP * (b + 1), :].rearrange("(p t) j -> p t j", t=PACK)
+            season_sb = staged([P, PACK, S], F32, "season_sb")
+            for tp in range(2):
+                nc.sync.dma_start(out=season_sb[:, 2 * tp : 2 * tp + 2, :], in_=rows[:, 2 * tp : 2 * tp + 2, :])
+            for jh in range(2):
+                jc = slice(JH * jh, JH * (jh + 1))
+                hb = ring.tile([P, PACK, JH], BF16, name="hb", align_bytes=64)
+                for tp in range(2):
+                    b1 = psum.tile([P, 2, JH], F32, name="acc1")
+                    b2 = psum.tile([P, 2, JH], F32, name="acc2")
+                    for a in range(PASSES):
+                        for u in range(2):
+                            cols = slice(P * (2 * tp + u), P * (2 * tp + u + 1))
+                            nc.tensor.matmul_mx(
+                                out=b1[:, u, :], lhsT=w1w[a][:, cols].bitcast(FP8X4), lhsT_scale=w1s[a][:, cols],
+                                rhs=vw[a][:, jc].bitcast(FP8X4), rhs_scale=vs[4 * a :, jc],
+                                start=(a == 0 and u == 0), stop=(a == PASSES - 1 and u == 1),
+                            )
+                    for a in range(PASSES):
+                        for u in range(2):
+                            c0 = KP * b + P * (2 * tp + u)
+                            nc.tensor.matmul_mx(
+                                out=b2[:, u, :], lhsT=w2w[:, H * a + c0 : H * a + c0 + P].bitcast(FP4X4),
+                                lhsT_scale=w2s[:, H * a + c0 : H * a + c0 + P],
+                                rhs=vw[a][:, jc].bitcast(FP8X4), rhs_scale=vs_low[a][:, jc],
+                                start=(a == 0 and u == 0), stop=(a == PASSES - 1 and u == 1),
+                            )
+                    bent = ring.tile([P, 2, JH], F32, name="bent")
+                    nc.vector.tensor_tensor(bent[:], b1[:], season_sb[:, 2 * tp : 2 * tp + 2, jc], MULT)
+                    th = ring.tile([P, 2, JH], F32, name="th")
+                    nc.scalar.activation(th[:], bent[:], TANH)
+                    for u in range(2):
+                        t = 2 * tp + u
+                        nc.vector.scalar_tensor_tensor(
+                            hb[:, t, :], th[:, u, :], gain_sb[:, b, t : t + 1], b2[:, u, :], MULT, ADD
+                        )
+                hi = ring.tile([P, JH, PACK], BF16, name="hi", align_bytes=64)
+                dst = hi[:].rearrange("p (c i) t -> p c t i", i=4)
+                src = hb[:].rearrange("p t (c i) -> p c t i", i=4)
+                if b == 0:
+                    nc.vector.tensor_copy(out=dst, in_=src)
+                else:
+                    nc.scalar.copy(out=dst, in_=src)
+                h_words[b, jh] = keep([P, JH], U32, "hw%d%d" % (b, jh))
+                h_scales[b, jh] = keep([P, JH], U8, "hs%d%d" % (b, jh))
+                nc.vector.quantize_mx(
+                    out=h_words[b, jh][:].bitcast(FP8X4), scales=h_scales[b, jh][:],
+                    in_=hi[:].rearrange("p j t -> p (j t)"),
+                )
+
+        wgo_sb = ring.tile([P, S], F32, name="wgo_sb", tag="grouped", bufs=2, align_bytes=64)
+        nc.sync.dma_start(out=wgo_sb[:], in_=wgo)
+        page = [staged([P, T2], F32, "page%d" % c) for c in range(S2 // P)]
+        for c in range(S2 // P):
+            nc.sync.dma_start(out=page[c][:], in_=page1[P * c : P * (c + 1), :])
+
+        for jh in range(2):
+            jc = slice(JH * jh, JH * (jh + 1))
+            for cp in range(2):
+                e = psum.tile([P, 2, JH], F32, name="acc1")
+                for b in range(PASSES):
+                    for u in range(2):
+                        cols = slice(P * (2 * cp + u), P * (2 * cp + u + 1))
+                        nc.tensor.matmul_mx(
+                            out=e[:, u, :], lhsT=v2w[b][:, cols].bitcast(FP8X4), lhsT_scale=v2s[4 * b :, cols],
+                            rhs=h_words[b, jh][:].bitcast(FP8X4), rhs_scale=h_scales[b, jh][:],
+                            start=(b == 0 and u == 0), stop=(b == PASSES - 1 and u == 1),
+                        )
+                z = ring.tile([P, 2, JH], F32, name="z")
+                for u in range(2):
+                    c = 2 * cp + u
+                    nc.vector.scalar_tensor_tensor(
+                        z[:, u, :], e[:, u, :], ex_sb[:, c : c + 1], d_sb[c][:, jc], MULT, ADD
+                    )
+                for u in range(2):
+                    c = 2 * cp + u
+                    y = ring.tile([P, JH], F32, name="y", bufs=4)
+                    nc.scalar.activation(y[:], z[:, u, :], TANH)
+                    nc.vector.tensor_tensor(
+                        page[c][:].indirect(lst3[:, (JH // 16) * jh : (JH // 16) * (jh + 1)]), y[:], wgo_sb[:, jc], MULT
+                    )
+                    if jh == 1:
+                        nc.sync.dma_start(out=out[P * c : P * (c + 1), :], in_=page[c][:])

@@ -46,13 +46,28 @@ def tile_list_star_conference_scores_kernel(
         lst2 = keep([P, S2 // 16], U16, "lst2")
         lst3 = keep([P, S // 16], U16, "lst3")
 
-        def load_scales(dram, plane):
-            nc.gpsimd.memset(plane[:].bitcast(I32), 0)
+        def load_scales(engine, dram, plane):
             for q in range(4):
-                nc.scalar.dma_start(
+                engine.dma_start(
                     out=plane[32 * q : 32 * q + 8, :].bitcast(I32),
                     in_=dram[:, 4 * q : 4 * q + 4, :].bitcast(I32),
                 )
+
+        def plane_down(src, width, name):
+            low = keep([P, width], U8, name)
+            nc.vector.memset(low[:].bitcast(I32), 0)
+            nc.gpsimd.dma_start(out=low[0:112, :].bitcast(I32), in_=src[4:116, :].bitcast(I32))
+            return low
+
+        tabs = keep([P, T], U8, "tabs")
+        tab2s = keep([P, T3], U8, "tab2s")
+        w2s_raw = held.tile([P, H], U8, name="w2s_raw", tag="w2s_raw", align_bytes=64)
+        nc.gpsimd.memset(tabs[:].bitcast(I32), 0)
+        nc.vector.memset(tab2s[:].bitcast(I32), 0)
+        nc.vector.memset(w2s_raw[:].bitcast(I32), 0)
+        load_scales(nc.scalar, tab_scales, tabs)
+        load_scales(nc.gpsimd, tab2_scales, tab2s)
+        load_scales(nc.gpsimd, w2_scales, w2s_raw)
 
         nc.sync.dma_start(lst[:], offs)
         nc.sync.dma_start(lst2[:], offs2)
@@ -62,31 +77,6 @@ def tile_list_star_conference_scores_kernel(
             nc.sync.dma_start(
                 out=tabw[a][:].bitcast(I32), in_=tab_words[a].rearrange("p t i -> p (t i)").bitcast(I32)
             )
-        tabs = staged([P, T], U8, "tabs")
-        load_scales(tab_scales, tabs)
-        tab2s = staged([P, T3], U8, "tab2s")
-        load_scales(tab2_scales, tab2s)
-        w2s_raw = held.tile([P, PASSES * H], U8, name="w2s_raw", tag="w2s_raw", align_bytes=64)
-        nc.gpsimd.memset(w2s_raw[:].bitcast(I32), 0)
-        for q in range(4):
-            nc.scalar.dma_start(
-                out=w2s_raw[32 * q : 32 * q + 4, :].bitcast(I32).rearrange("r (a c) -> r a c", a=PASSES),
-                in_=w2_scales[:, 4 * q : 4 * q + 4, :].bitcast(I32).rearrange("a r c -> r a c"),
-            )
-
-        vs = keep([P, S], U8, "vs")
-        nc.vector.tensor_copy(vs[:], tabs[:].indirect(lst[:]))
-        vs1 = keep([P, S], U8, "vs1")
-        nc.gpsimd.memset(vs1[:].bitcast(I32), 0)
-        nc.scalar.dma_start(out=vs1[0:112, :].bitcast(I32), in_=vs[4:116, :].bitcast(I32))
-        vs_low = [vs, vs1]
-        vw = [keep([P, S], U32, "vw%d" % a) for a in range(PASSES)]
-        v2w = [keep([P, S2], U32, "v2w%d" % a) for a in range(PASSES)]
-        v2s = keep([P, S2], U8, "v2s")
-        for a in range(PASSES):
-            nc.vector.tensor_copy(vw[a][:], tabw[a][:].indirect(lst[:]))
-        nc.vector.tensor_copy(v2s[:], tab2s[:].indirect(lst2[:]))
-
         tab2w = staged([P, PASSES * T3], U32, "tab2w")
         nc.sync.dma_start(
             out=tab2w[:].bitcast(I32).rearrange("p (a c) -> p a c", a=PASSES),
@@ -97,13 +87,24 @@ def tile_list_star_conference_scores_kernel(
             out=w2_raw[:].bitcast(I32).rearrange("p (a c) -> p a c", a=PASSES),
             in_=w2_words.rearrange("a p c -> p a c").bitcast(I32),
         )
+
+        vs = keep([P, S], U8, "vs")
+        nc.vector.tensor_copy(vs[:], tabs[:].indirect(lst[:]))
+        vs_low = [vs, plane_down(vs, S, "vs1")]
+        vw = [keep([P, S], U32, "vw%d" % a) for a in range(PASSES)]
+        v2w = [keep([P, S2], U32, "v2w%d" % a) for a in range(PASSES)]
+        v2s = keep([P, S2], U8, "v2s")
+        for a in range(PASSES):
+            nc.vector.tensor_copy(vw[a][:], tabw[a][:].indirect(lst[:]))
+        nc.vector.tensor_copy(v2s[:], tab2s[:].indirect(lst2[:]))
         for a in range(PASSES):
             nc.vector.tensor_copy(v2w[a][:], tab2w[:, T3 * a : T3 * (a + 1)].indirect(lst2[:]))
-        w2s = keep([P, PASSES * H], U8, "w2s")
+        w2s = keep([P, H], U8, "w2s")
         nc.vector.tensor_copy(
             out=w2s[:].rearrange("p (g t m) -> p g t m", t=PACK, m=P),
             in_=w2s_raw[:].rearrange("p (g m t) -> p g t m", t=PACK, m=P),
         )
+        w2s_low = [w2s, plane_down(w2s, H, "w2s1")]
 
         factors = held.tile([P, 16], F32, name="factors", tag="w2s_raw", align_bytes=64)
         gain_sb = factors[:, 0:8].rearrange("p (b t) -> p b t", b=PASSES)
@@ -130,78 +131,88 @@ def tile_list_star_conference_scores_kernel(
             in_=w2_raw[:].rearrange("p (g m t) -> p g t m", t=PACK, m=P),
         )
 
+        def quantize_w1(a, b):
+            raw = staged([P, PACK, KP], F32, "w1_raw")
+            nc.sync.dma_start(
+                out=raw[:],
+                in_=w1[KP * a : KP * (a + 1), KP * b : KP * (b + 1)].rearrange("(p j) c -> p j c", j=PACK),
+            )
+            grouped = ring.tile([P, PACK, P, PACK], BF16, name="grouped", tag="grouped", bufs=2, align_bytes=64)
+            dst = grouped[:].rearrange("p t m j -> p m j t")
+            src = raw[:].rearrange("p j (m t) -> p m j t", t=PACK)
+            cut = SCALAR_SHARE[a, b]
+            if cut > 0:
+                nc.scalar.copy(out=dst[:, :cut], in_=src[:, :cut])
+            if cut < P:
+                nc.vector.tensor_copy(out=dst[:, cut:], in_=src[:, cut:])
+            words = keep([P, KP], U32, "w1w%d%d" % (a, b))
+            scales = keep([P, KP], U8, "w1s%d%d" % (a, b))
+            nc.vector.quantize_mx(
+                out=words[:].bitcast(FP8X4), scales=scales[:], in_=grouped[:].rearrange("p t m j -> p (t m j)")
+            )
+            return words, scales
+
+        def make_h(b, w1q, season_sb, j0, nj, weave):
+            jc = slice(j0, j0 + nj)
+            nt = S // nj
+            hb = keep([P, PACK, nj], BF16, "hb%d_%d" % (b, j0))
+            for t0 in range(0, PACK, nt):
+                b1 = psum.tile([P, nt, nj], F32, name="acc1")
+                b2 = psum.tile([P, nt, nj], F32, name="acc2")
+                for a in range(PASSES):
+                    for u in range(nt):
+                        cols = slice(P * (t0 + u), P * (t0 + u + 1))
+                        nc.tensor.matmul_mx(
+                            out=b1[:, u, :], lhsT=w1q[a][0][:, cols].bitcast(FP8X4), lhsT_scale=w1q[a][1][:, cols],
+                            rhs=vw[a][:, jc].bitcast(FP8X4), rhs_scale=vs[4 * a :, jc],
+                            start=(a == 0 and u == 0), stop=(a == PASSES - 1 and u == nt - 1),
+                        )
+                for a in range(PASSES):
+                    for u in range(nt):
+                        c0 = KP * b + P * (t0 + u)
+                        nc.tensor.matmul_mx(
+                            out=b2[:, u, :], lhsT=w2w[:, H * a + c0 : H * a + c0 + P].bitcast(FP4X4),
+                            lhsT_scale=w2s_low[a][:, c0 : c0 + P],
+                            rhs=vw[a][:, jc].bitcast(FP8X4), rhs_scale=vs_low[a][:, jc],
+                            start=(a == 0 and u == 0), stop=(a == PASSES - 1 and u == nt - 1),
+                        )
+                bent = ring.tile([P, nt, nj], F32, name="bent")
+                nc.vector.tensor_tensor(bent[:], b1[:], season_sb[:, t0 : t0 + nt, jc], MULT)
+                th = ring.tile([P, nt, nj], F32, name="th")
+                nc.scalar.activation(th[:], bent[:], TANH)
+                for u in range(nt):
+                    t = t0 + u
+                    nc.vector.scalar_tensor_tensor(
+                        hb[:, t, :], th[:, u, :], gain_sb[:, b, t : t + 1], b2[:, u, :], MULT, ADD
+                    )
+            hi = keep([P, nj, PACK], BF16, "hi%d_%d" % (b, j0))
+            weave(hi[:].rearrange("p (c i) t -> p c t i", i=4), hb[:].rearrange("p t (c i) -> p c t i", i=4))
+            words = keep([P, nj], U32, "hw%d_%d" % (b, j0))
+            scales = keep([P, nj], U8, "hs%d_%d" % (b, j0))
+            nc.vector.quantize_mx(
+                out=words[:].bitcast(FP8X4), scales=scales[:], in_=hi[:].rearrange("p j t -> p (j t)")
+            )
+            return words, scales
+
+        def load_season(b):
+            rows = season[KP * b : KP * (b + 1), :].rearrange("(p t) j -> p t j", t=PACK)
+            tile = staged([P, PACK, S], F32, "season_sb")
+            for tp in range(2):
+                nc.sync.dma_start(out=tile[:, 2 * tp : 2 * tp + 2, :], in_=rows[:, 2 * tp : 2 * tp + 2, :])
+            return tile
+
+        w1q = [quantize_w1(a, 0) for a in range(PASSES)]
+        h0_words, h0_scales = make_h(0, w1q, load_season(0), 0, S, nc.vector.tensor_copy)
+        w1q = [quantize_w1(a, 1) for a in range(PASSES)]
+        season_sb = load_season(1)
+        h1 = [make_h(1, w1q, season_sb, JH * jh, JH, nc.scalar.copy) for jh in range(2)]
         h_words = {}
         h_scales = {}
-        for b in range(PASSES):
-            w1w, w1s = [], []
-            for a in range(PASSES):
-                w1_raw = staged([P, PACK, KP], F32, "w1_raw")
-                nc.sync.dma_start(
-                    out=w1_raw[:],
-                    in_=w1[KP * a : KP * (a + 1), KP * b : KP * (b + 1)].rearrange("(p j) c -> p j c", j=PACK),
-                )
-                grouped = ring.tile([P, PACK, P, PACK], BF16, name="grouped", tag="grouped", bufs=2, align_bytes=64)
-                dst = grouped[:].rearrange("p t m j -> p m j t")
-                src = w1_raw[:].rearrange("p j (m t) -> p m j t", t=PACK)
-                cut = SCALAR_SHARE[a, b]
-                nc.scalar.copy(out=dst[:, :cut], in_=src[:, :cut])
-                if cut < P:
-                    nc.vector.tensor_copy(out=dst[:, cut:], in_=src[:, cut:])
-                w1w.append(keep([P, KP], U32, "w1w%d%d" % (a, b)))
-                w1s.append(keep([P, KP], U8, "w1s%d%d" % (a, b)))
-                nc.vector.quantize_mx(
-                    out=w1w[a][:].bitcast(FP8X4), scales=w1s[a][:],
-                    in_=grouped[:].rearrange("p t m j -> p (t m j)"),
-                )
-            rows = season[KP * b : KP * (b + 1), :].rearrange("(p t) j -> p t j", t=PACK)
-            season_sb = staged([P, PACK, S], F32, "season_sb")
-            for tp in range(2):
-                nc.sync.dma_start(out=season_sb[:, 2 * tp : 2 * tp + 2, :], in_=rows[:, 2 * tp : 2 * tp + 2, :])
-            for jh in range(2):
-                jc = slice(JH * jh, JH * (jh + 1))
-                hb = ring.tile([P, PACK, JH], BF16, name="hb", align_bytes=64)
-                for tp in range(2):
-                    b1 = psum.tile([P, 2, JH], F32, name="acc1")
-                    b2 = psum.tile([P, 2, JH], F32, name="acc2")
-                    for a in range(PASSES):
-                        for u in range(2):
-                            cols = slice(P * (2 * tp + u), P * (2 * tp + u + 1))
-                            nc.tensor.matmul_mx(
-                                out=b1[:, u, :], lhsT=w1w[a][:, cols].bitcast(FP8X4), lhsT_scale=w1s[a][:, cols],
-                                rhs=vw[a][:, jc].bitcast(FP8X4), rhs_scale=vs[4 * a :, jc],
-                                start=(a == 0 and u == 0), stop=(a == PASSES - 1 and u == 1),
-                            )
-                    for a in range(PASSES):
-                        for u in range(2):
-                            c0 = KP * b + P * (2 * tp + u)
-                            nc.tensor.matmul_mx(
-                                out=b2[:, u, :], lhsT=w2w[:, H * a + c0 : H * a + c0 + P].bitcast(FP4X4),
-                                lhsT_scale=w2s[:, H * a + c0 : H * a + c0 + P],
-                                rhs=vw[a][:, jc].bitcast(FP8X4), rhs_scale=vs_low[a][:, jc],
-                                start=(a == 0 and u == 0), stop=(a == PASSES - 1 and u == 1),
-                            )
-                    bent = ring.tile([P, 2, JH], F32, name="bent")
-                    nc.vector.tensor_tensor(bent[:], b1[:], season_sb[:, 2 * tp : 2 * tp + 2, jc], MULT)
-                    th = ring.tile([P, 2, JH], F32, name="th")
-                    nc.scalar.activation(th[:], bent[:], TANH)
-                    for u in range(2):
-                        t = 2 * tp + u
-                        nc.vector.scalar_tensor_tensor(
-                            hb[:, t, :], th[:, u, :], gain_sb[:, b, t : t + 1], b2[:, u, :], MULT, ADD
-                        )
-                hi = ring.tile([P, JH, PACK], BF16, name="hi", align_bytes=64)
-                dst = hi[:].rearrange("p (c i) t -> p c t i", i=4)
-                src = hb[:].rearrange("p t (c i) -> p c t i", i=4)
-                if b == 0:
-                    nc.vector.tensor_copy(out=dst, in_=src)
-                else:
-                    nc.scalar.copy(out=dst, in_=src)
-                h_words[b, jh] = keep([P, JH], U32, "hw%d%d" % (b, jh))
-                h_scales[b, jh] = keep([P, JH], U8, "hs%d%d" % (b, jh))
-                nc.vector.quantize_mx(
-                    out=h_words[b, jh][:].bitcast(FP8X4), scales=h_scales[b, jh][:],
-                    in_=hi[:].rearrange("p j t -> p (j t)"),
-                )
+        for jh in range(2):
+            h_words[0, jh] = h0_words[:, JH * jh : JH * (jh + 1)]
+            h_scales[0, jh] = h0_scales[:, JH * jh : JH * (jh + 1)]
+            h_words[1, jh] = h1[jh][0][:]
+            h_scales[1, jh] = h1[jh][1][:]
 
         wgo_sb = ring.tile([P, S], F32, name="wgo_sb", tag="grouped", bufs=2, align_bytes=64)
         nc.sync.dma_start(out=wgo_sb[:], in_=wgo)
@@ -218,7 +229,7 @@ def tile_list_star_conference_scores_kernel(
                         cols = slice(P * (2 * cp + u), P * (2 * cp + u + 1))
                         nc.tensor.matmul_mx(
                             out=e[:, u, :], lhsT=v2w[b][:, cols].bitcast(FP8X4), lhsT_scale=v2s[4 * b :, cols],
-                            rhs=h_words[b, jh][:].bitcast(FP8X4), rhs_scale=h_scales[b, jh][:],
+                            rhs=h_words[b, jh].bitcast(FP8X4), rhs_scale=h_scales[b, jh],
                             start=(b == 0 and u == 0), stop=(b == PASSES - 1 and u == 1),
                         )
                 z = ring.tile([P, 2, JH], F32, name="z")

@@ -15,6 +15,7 @@ FP8X4 = mybir.dt.float8_e4m3fn_x4
 FP4X4 = mybir.dt.float4_e2m1fn_x4
 MULT = mybir.AluOpType.mult
 ADD = mybir.AluOpType.add
+COPY = mybir.ActivationFunctionType.Copy
 TANH = mybir.ActivationFunctionType.Tanh
 
 P = 128
@@ -22,7 +23,8 @@ PACK = 4
 KP = P * PACK
 PASSES = 2
 JH = S // 2
-SCALAR_SHARE = {(0, 0): 128, (1, 0): 40, (0, 1): 128, (1, 1): 40}
+REUSES = {"v2w0": "grouped11", "v2w1": "th1_0_2", "hw0_0": "bent1_0_0", "bent1_256_0": "hi1_0", "bent1_256_2": "hb1_0", "hi0_0": "w1_raw11"}
+SCALAR_SHARE = {(0, 0): 64, (1, 0): 48, (0, 1): 128, (1, 1): 64}
 
 
 def tile_list_star_conference_scores_kernel(
@@ -32,15 +34,11 @@ def tile_list_star_conference_scores_kernel(
     nc = tc.nc
     with ExitStack() as ctx:
         held = ctx.enter_context(tc.tile_pool(name="held", bufs=1))
-        ring = ctx.enter_context(tc.tile_pool(name="ring", bufs=3))
-        stage = ctx.enter_context(tc.tile_pool(name="stage", bufs=4))
+        ring = ctx.enter_context(tc.tile_pool(name="ring", bufs=8))
         psum = ctx.enter_context(tc.psum_pool(name="psum", bufs=4))
 
         def keep(shape, dtype, name):
-            return held.tile(shape, dtype, name=name, align_bytes=64)
-
-        def staged(shape, dtype, name):
-            return stage.tile(shape, dtype, name=name, tag="staged", align_bytes=64)
+            return held.tile(shape, dtype, name=name, tag=REUSES.get(name, name), align_bytes=64)
 
         lst = keep([P, S // 16], U16, "lst")
         lst2 = keep([P, S2 // 16], U16, "lst2")
@@ -49,97 +47,100 @@ def tile_list_star_conference_scores_kernel(
         def load_scales(engine, dram, plane):
             for q in range(4):
                 engine.dma_start(
+                    out=plane[32 * q : 32 * q + 4, :].bitcast(I32).rearrange("r (a c) -> r a c", a=PASSES),
+                    in_=dram[:, 4 * q : 4 * q + 4, :].bitcast(I32).rearrange("a r c -> r a c"),
+                )
+
+        def load_packed_scales(engine, dram, plane):
+            for q in range(4):
+                engine.dma_start(
                     out=plane[32 * q : 32 * q + 8, :].bitcast(I32),
                     in_=dram[:, 4 * q : 4 * q + 4, :].bitcast(I32),
                 )
 
-        def plane_down(src, width, name):
-            low = keep([P, width], U8, name)
-            nc.vector.memset(low[:].bitcast(I32), 0)
-            nc.gpsimd.dma_start(out=low[0:112, :].bitcast(I32), in_=src[4:116, :].bitcast(I32))
-            return low
-
-        tabs = keep([P, T], U8, "tabs")
+        tabs = keep([P, PASSES * T], U8, "tabs")
+        w2s_raw = keep([P, PASSES * H], U8, "w2s_raw")
         tab2s = keep([P, T3], U8, "tab2s")
-        w2s_raw = held.tile([P, H], U8, name="w2s_raw", tag="w2s_raw", align_bytes=64)
-        nc.gpsimd.memset(tabs[:].bitcast(I32), 0)
-        nc.vector.memset(tab2s[:].bitcast(I32), 0)
+        nc.gpsimd.memset(tabs[:, :T].bitcast(I32), 0)
+        nc.vector.memset(tabs[:, T:].bitcast(I32), 0)
         nc.vector.memset(w2s_raw[:].bitcast(I32), 0)
-        load_scales(nc.scalar, tab_scales, tabs)
-        load_scales(nc.gpsimd, tab2_scales, tab2s)
-        load_scales(nc.gpsimd, w2_scales, w2s_raw)
+        nc.gpsimd.memset(tab2s[:].bitcast(I32), 0)
+
+        w2_raw = keep([P, PASSES * H], U16, "w2_raw")
+        tabw = [keep([P, T], U32, "tabw%d" % a) for a in range(PASSES)]
+        tab2w = keep([P, PASSES * T3], U32, "tab2w")
+        gain_sb = keep([P, PASSES, PACK], F32, "gain_sb")
+        ex_sb = keep([P, S2 // P], F32, "ex_sb")
+        wgo_sb = keep([P, S], F32, "wgo_sb")
+        page = [keep([P, T2], F32, "page%d" % c) for c in range(S2 // P)]
+        w1_raw = {(a, b): keep([P, PACK, KP], F32, "w1_raw%d%d" % (a, b)) for a in range(PASSES) for b in range(PASSES)}
+        season_sb = [keep([P, PACK, S], F32, "season%d" % b) for b in range(PASSES)]
+
+        def load_words(a):
+            nc.sync.dma_start(out=tabw[a][:].bitcast(I32), in_=tab_words[a].rearrange("p t i -> p (t i)").bitcast(I32))
+
+        def load_w1(a, b):
+            nc.sync.dma_start(
+                out=w1_raw[a, b][:],
+                in_=w1[KP * a : KP * (a + 1), KP * b : KP * (b + 1)].rearrange("(p j) c -> p j c", j=PACK),
+            )
+
+        def load_season(b):
+            rows = season[KP * b : KP * (b + 1), :].rearrange("(p t) j -> p t j", t=PACK)
+            for tp in range(2):
+                nc.sync.dma_start(out=season_sb[b][:, 2 * tp : 2 * tp + 2, :], in_=rows[:, 2 * tp : 2 * tp + 2, :])
 
         nc.sync.dma_start(lst[:], offs)
-        nc.sync.dma_start(lst2[:], offs2)
-        nc.sync.dma_start(lst3[:], offs3)
-        tabw = [staged([P, T], U32, "tabw%d" % a) for a in range(PASSES)]
-        for a in range(PASSES):
-            nc.sync.dma_start(
-                out=tabw[a][:].bitcast(I32), in_=tab_words[a].rearrange("p t i -> p (t i)").bitcast(I32)
-            )
-        tab2w = staged([P, PASSES * T3], U32, "tab2w")
-        nc.sync.dma_start(
-            out=tab2w[:].bitcast(I32).rearrange("p (a c) -> p a c", a=PASSES),
-            in_=tab2_words.rearrange("a p t i -> p a (t i)").bitcast(I32),
-        )
-        w2_raw = staged([P, PASSES * H], U16, "w2_raw")
         nc.sync.dma_start(
             out=w2_raw[:].bitcast(I32).rearrange("p (a c) -> p a c", a=PASSES),
             in_=w2_words.rearrange("a p c -> p a c").bitcast(I32),
         )
-
-        vs = keep([P, S], U8, "vs")
-        nc.vector.tensor_copy(vs[:], tabs[:].indirect(lst[:]))
-        vs_low = [vs, plane_down(vs, S, "vs1")]
-        vw = [keep([P, S], U32, "vw%d" % a) for a in range(PASSES)]
-        v2w = [keep([P, S2], U32, "v2w%d" % a) for a in range(PASSES)]
-        v2s = keep([P, S2], U8, "v2s")
-        for a in range(PASSES):
-            nc.vector.tensor_copy(vw[a][:], tabw[a][:].indirect(lst[:]))
-        nc.vector.tensor_copy(v2s[:], tab2s[:].indirect(lst2[:]))
-        for a in range(PASSES):
-            nc.vector.tensor_copy(v2w[a][:], tab2w[:, T3 * a : T3 * (a + 1)].indirect(lst2[:]))
-        w2s = keep([P, H], U8, "w2s")
-        nc.vector.tensor_copy(
-            out=w2s[:].rearrange("p (g t m) -> p g t m", t=PACK, m=P),
-            in_=w2s_raw[:].rearrange("p (g m t) -> p g t m", t=PACK, m=P),
+        load_scales(nc.sync, tab_scales, tabs)
+        load_words(0)
+        load_words(1)
+        load_scales(nc.sync, w2_scales, w2s_raw)
+        load_w1(0, 0)
+        nc.sync.dma_start(out=gain_sb[:], in_=gain.rearrange("(b p t) -> p b t", b=PASSES, t=PACK))
+        load_w1(1, 0)
+        load_season(0)
+        load_w1(0, 1)
+        nc.sync.dma_start(lst2[:], offs2)
+        load_packed_scales(nc.sync, tab2_scales, tab2s)
+        load_w1(1, 1)
+        nc.sync.dma_start(
+            out=tab2w[:].bitcast(I32).rearrange("p (a c) -> p a c", a=PASSES),
+            in_=tab2_words.rearrange("a p t i -> p a (t i)").bitcast(I32),
         )
-        w2s_low = [w2s, plane_down(w2s, H, "w2s1")]
-
-        factors = held.tile([P, 16], F32, name="factors", tag="w2s_raw", align_bytes=64)
-        gain_sb = factors[:, 0:8].rearrange("p (b t) -> p b t", b=PASSES)
-        ex_sb = factors[:, 8:12]
-        nc.sync.dma_start(out=gain_sb, in_=gain.rearrange("(b p t) -> p b t", b=PASSES, t=PACK))
+        load_season(1)
+        nc.sync.dma_start(lst3[:], offs3)
         with nc.allow_non_contiguous_dma(reason="one value a partition"):
-            nc.sync.dma_start(out=ex_sb, in_=ex.rearrange("(c p) -> p c", p=P))
-
-        d_sb = []
+            nc.sync.dma_start(out=ex_sb[:], in_=ex.rearrange("(c p) -> p c", p=P))
+        nc.sync.dma_start(out=wgo_sb[:], in_=wgo)
         for c in range(S2 // P):
-            cols = slice(P * c, P * (c + 1))
-            acc = psum.tile([P, S], F32, name="acc2")
-            for a in range(PASSES):
-                nc.tensor.matmul_mx(
-                    out=acc[:], lhsT=v2w[a][:, cols].bitcast(FP8X4), lhsT_scale=v2s[4 * a :, cols],
-                    rhs=vw[a][:].bitcast(FP8X4), rhs_scale=vs[4 * a :, :], start=(a == 0), stop=(a == PASSES - 1),
-                )
-            d_sb.append(keep([P, S], F32, "d_sb%d" % c))
-            nc.scalar.copy(out=d_sb[c][:], in_=acc[:])
+            nc.sync.dma_start(out=page[c][:], in_=page1[P * c : P * (c + 1), :])
 
         w2w = keep([P, PASSES * H], U16, "w2w")
         nc.vector.tensor_copy(
             out=w2w[:].rearrange("p (g t m) -> p g t m", t=PACK, m=P),
             in_=w2_raw[:].rearrange("p (g m t) -> p g t m", t=PACK, m=P),
         )
+        vs = keep([P, PASSES, S], U8, "vs")
+        for a in range(PASSES):
+            nc.vector.tensor_copy(vs[:, a, :], tabs[:, T * a : T * (a + 1)].indirect(lst[:]))
+        vw = [keep([P, S], U32, "vw%d" % a) for a in range(PASSES)]
+        for a in range(PASSES):
+            nc.vector.tensor_copy(vw[a][:], tabw[a][:].indirect(lst[:]))
+        w2s = keep([P, PASSES * H], U8, "w2s")
+        nc.vector.tensor_copy(
+            out=w2s[:].rearrange("p (g t m) -> p g t m", t=PACK, m=P),
+            in_=w2s_raw[:].rearrange("p (g m t) -> p g t m", t=PACK, m=P),
+        )
+
 
         def quantize_w1(a, b):
-            raw = staged([P, PACK, KP], F32, "w1_raw")
-            nc.sync.dma_start(
-                out=raw[:],
-                in_=w1[KP * a : KP * (a + 1), KP * b : KP * (b + 1)].rearrange("(p j) c -> p j c", j=PACK),
-            )
-            grouped = ring.tile([P, PACK, P, PACK], BF16, name="grouped", tag="grouped", bufs=2, align_bytes=64)
+            grouped = keep([P, PACK, P, PACK], BF16, "grouped%d%d" % (a, b))
             dst = grouped[:].rearrange("p t m j -> p m j t")
-            src = raw[:].rearrange("p j (m t) -> p m j t", t=PACK)
+            src = w1_raw[a, b][:].rearrange("p j (m t) -> p m j t", t=PACK)
             cut = SCALAR_SHARE[a, b]
             if cut > 0:
                 nc.scalar.copy(out=dst[:, :cut], in_=src[:, :cut])
@@ -147,46 +148,64 @@ def tile_list_star_conference_scores_kernel(
                 nc.vector.tensor_copy(out=dst[:, cut:], in_=src[:, cut:])
             words = keep([P, KP], U32, "w1w%d%d" % (a, b))
             scales = keep([P, KP], U8, "w1s%d%d" % (a, b))
-            nc.vector.quantize_mx(
-                out=words[:].bitcast(FP8X4), scales=scales[:], in_=grouped[:].rearrange("p t m j -> p (t m j)")
-            )
+            parts = 1 + a
+            for i in range(parts):
+                ts = slice(PACK // parts * i, PACK // parts * (i + 1))
+                cols = slice(KP // parts * i, KP // parts * (i + 1))
+                nc.vector.quantize_mx(
+                    out=words[:, cols].bitcast(FP8X4), scales=scales[:, cols],
+                    in_=grouped[:, ts].rearrange("p t m j -> p (t m j)"),
+                )
             return words, scales
 
-        def make_h(b, w1q, season_sb, j0, nj, weave):
+        def bend(b, w1q, j0, nj):
             jc = slice(j0, j0 + nj)
             nt = S // nj
-            hb = keep([P, PACK, nj], BF16, "hb%d_%d" % (b, j0))
+            tanhs = []
             for t0 in range(0, PACK, nt):
                 b1 = psum.tile([P, nt, nj], F32, name="acc1")
-                b2 = psum.tile([P, nt, nj], F32, name="acc2")
                 for a in range(PASSES):
                     for u in range(nt):
                         cols = slice(P * (t0 + u), P * (t0 + u + 1))
                         nc.tensor.matmul_mx(
                             out=b1[:, u, :], lhsT=w1q[a][0][:, cols].bitcast(FP8X4), lhsT_scale=w1q[a][1][:, cols],
-                            rhs=vw[a][:, jc].bitcast(FP8X4), rhs_scale=vs[4 * a :, jc],
+                            rhs=vw[a][:, jc].bitcast(FP8X4), rhs_scale=vs[:, a, jc],
                             start=(a == 0 and u == 0), stop=(a == PASSES - 1 and u == nt - 1),
                         )
+                bent = keep([P, nt, nj], F32, "bent%d_%d_%d" % (b, j0, t0))
+                nc.vector.tensor_tensor(bent[:], b1[:], season_sb[b][:, t0 : t0 + nt, jc], MULT)
+                th = keep([P, nt, nj], F32, "th%d_%d_%d" % (b, j0, t0))
+                nc.scalar.activation(th[:], bent[:], TANH)
+                tanhs.append(th)
+            return tanhs
+
+        def join(b, tanhs, j0, nj):
+            jc = slice(j0, j0 + nj)
+            nt = S // nj
+            hb = keep([P, PACK, nj], BF16, "hb%d_%d" % (b, j0))
+            for t0 in range(0, PACK, nt):
+                b2 = psum.tile([P, nt, nj], F32, name="acc2")
                 for a in range(PASSES):
                     for u in range(nt):
-                        c0 = KP * b + P * (t0 + u)
+                        c0 = H * a + KP * b + P * (t0 + u)
                         nc.tensor.matmul_mx(
-                            out=b2[:, u, :], lhsT=w2w[:, H * a + c0 : H * a + c0 + P].bitcast(FP4X4),
-                            lhsT_scale=w2s_low[a][:, c0 : c0 + P],
-                            rhs=vw[a][:, jc].bitcast(FP8X4), rhs_scale=vs_low[a][:, jc],
+                            out=b2[:, u, :], lhsT=w2w[:, c0 : c0 + P].bitcast(FP4X4), lhsT_scale=w2s[:, c0 : c0 + P],
+                            rhs=vw[a][:, jc].bitcast(FP8X4), rhs_scale=vs[:, a, jc],
                             start=(a == 0 and u == 0), stop=(a == PASSES - 1 and u == nt - 1),
                         )
-                bent = ring.tile([P, nt, nj], F32, name="bent")
-                nc.vector.tensor_tensor(bent[:], b1[:], season_sb[:, t0 : t0 + nt, jc], MULT)
-                th = ring.tile([P, nt, nj], F32, name="th")
-                nc.scalar.activation(th[:], bent[:], TANH)
                 for u in range(nt):
                     t = t0 + u
                     nc.vector.scalar_tensor_tensor(
-                        hb[:, t, :], th[:, u, :], gain_sb[:, b, t : t + 1], b2[:, u, :], MULT, ADD
+                        hb[:, t, :], tanhs[t0 // nt][:, u, :], gain_sb[:, b, t : t + 1], b2[:, u, :], MULT, ADD
                     )
+            return hb
+
+        def quantize_h(hb, b, j0, nj, weave):
             hi = keep([P, nj, PACK], BF16, "hi%d_%d" % (b, j0))
-            weave(hi[:].rearrange("p (c i) t -> p c t i", i=4), hb[:].rearrange("p t (c i) -> p c t i", i=4))
+            dst = hi[:].rearrange("p (c i) t -> p c t i", i=4)
+            src = hb[:].rearrange("p t (c i) -> p c t i", i=4)
+            for c0 in range(0, nj // 4, JH // 4):
+                weave(dst[:, c0 : c0 + JH // 4], src[:, c0 : c0 + JH // 4])
             words = keep([P, nj], U32, "hw%d_%d" % (b, j0))
             scales = keep([P, nj], U8, "hs%d_%d" % (b, j0))
             nc.vector.quantize_mx(
@@ -194,33 +213,8 @@ def tile_list_star_conference_scores_kernel(
             )
             return words, scales
 
-        def load_season(b):
-            rows = season[KP * b : KP * (b + 1), :].rearrange("(p t) j -> p t j", t=PACK)
-            tile = staged([P, PACK, S], F32, "season_sb")
-            for tp in range(2):
-                nc.sync.dma_start(out=tile[:, 2 * tp : 2 * tp + 2, :], in_=rows[:, 2 * tp : 2 * tp + 2, :])
-            return tile
-
-        w1q = [quantize_w1(a, 0) for a in range(PASSES)]
-        h0_words, h0_scales = make_h(0, w1q, load_season(0), 0, S, nc.vector.tensor_copy)
-        w1q = [quantize_w1(a, 1) for a in range(PASSES)]
-        season_sb = load_season(1)
-        h1 = [make_h(1, w1q, season_sb, JH * jh, JH, nc.scalar.copy) for jh in range(2)]
-        h_words = {}
-        h_scales = {}
-        for jh in range(2):
-            h_words[0, jh] = h0_words[:, JH * jh : JH * (jh + 1)]
-            h_scales[0, jh] = h0_scales[:, JH * jh : JH * (jh + 1)]
-            h_words[1, jh] = h1[jh][0][:]
-            h_scales[1, jh] = h1[jh][1][:]
-
-        wgo_sb = ring.tile([P, S], F32, name="wgo_sb", tag="grouped", bufs=2, align_bytes=64)
-        nc.sync.dma_start(out=wgo_sb[:], in_=wgo)
-        page = [staged([P, T2], F32, "page%d" % c) for c in range(S2 // P)]
-        for c in range(S2 // P):
-            nc.sync.dma_start(out=page[c][:], in_=page1[P * c : P * (c + 1), :])
-
-        for jh in range(2):
+        def score(jh, h1q):
+            hq = [(h0_words[:, JH * jh : JH * (jh + 1)], h0_scales[:, JH * jh : JH * (jh + 1)]), (h1q[0][:], h1q[1][:])]
             jc = slice(JH * jh, JH * (jh + 1))
             for cp in range(2):
                 e = psum.tile([P, 2, JH], F32, name="acc1")
@@ -229,15 +223,24 @@ def tile_list_star_conference_scores_kernel(
                         cols = slice(P * (2 * cp + u), P * (2 * cp + u + 1))
                         nc.tensor.matmul_mx(
                             out=e[:, u, :], lhsT=v2w[b][:, cols].bitcast(FP8X4), lhsT_scale=v2s[4 * b :, cols],
-                            rhs=h_words[b, jh].bitcast(FP8X4), rhs_scale=h_scales[b, jh],
+                            rhs=hq[b][0].bitcast(FP8X4), rhs_scale=hq[b][1],
                             start=(b == 0 and u == 0), stop=(b == PASSES - 1 and u == 1),
                         )
-                z = ring.tile([P, 2, JH], F32, name="z")
+                d = psum.tile([P, 2, JH], F32, name="acc2")
+                for a in range(PASSES):
+                    for u in range(2):
+                        cols = slice(P * (2 * cp + u), P * (2 * cp + u + 1))
+                        nc.tensor.matmul_mx(
+                            out=d[:, u, :], lhsT=v2w[a][:, cols].bitcast(FP8X4), lhsT_scale=v2s[4 * a :, cols],
+                            rhs=vw[a][:, jc].bitcast(FP8X4), rhs_scale=vs[:, a, jc],
+                            start=(a == 0 and u == 0), stop=(a == PASSES - 1 and u == 1),
+                        )
+                scaled = ring.tile([P, 2, JH], F32, name="scaled")
                 for u in range(2):
                     c = 2 * cp + u
-                    nc.vector.scalar_tensor_tensor(
-                        z[:, u, :], e[:, u, :], ex_sb[:, c : c + 1], d_sb[c][:, jc], MULT, ADD
-                    )
+                    nc.scalar.activation(scaled[:, u, :], e[:, u, :], COPY, scale=ex_sb[:, c : c + 1])
+                z = ring.tile([P, 2, JH], F32, name="z")
+                nc.vector.tensor_tensor(z[:], scaled[:], d[:], ADD)
                 for u in range(2):
                     c = 2 * cp + u
                     y = ring.tile([P, JH], F32, name="y", bufs=4)
@@ -247,3 +250,22 @@ def tile_list_star_conference_scores_kernel(
                     )
                     if jh == 1:
                         nc.sync.dma_start(out=out[P * c : P * (c + 1), :], in_=page[c][:])
+
+        w1q0 = [quantize_w1(a, 0) for a in range(PASSES)]
+        th0 = bend(0, w1q0, 0, S)
+        w1q1 = [quantize_w1(a, 1) for a in range(PASSES)]
+        hb0 = join(0, th0, 0, S)
+        th10 = bend(1, w1q1, 0, JH)
+        hb10 = join(1, th10, 0, JH)
+        h0_words, h0_scales = quantize_h(hb0, 0, 0, S, nc.scalar.copy)
+        v2w = [keep([P, S2], U32, "v2w%d" % a) for a in range(PASSES)]
+        v2s = keep([P, S2], U8, "v2s")
+        nc.vector.tensor_copy(v2s[:], tab2s[:].indirect(lst2[:]))
+        for a in range(PASSES):
+            nc.vector.tensor_copy(v2w[a][:], tab2w[:, T3 * a : T3 * (a + 1)].indirect(lst2[:]))
+        h1 = [quantize_h(hb10, 1, 0, JH, nc.scalar.copy)]
+        th11 = bend(1, w1q1, JH, JH)
+        hb11 = join(1, th11, JH, JH)
+        h1.append(quantize_h(hb11, 1, JH, JH, nc.scalar.copy))
+        score(0, h1[0])
+        score(1, h1[1])

@@ -45,10 +45,10 @@ def tile_list_star_conference_scores_kernel(
         lst3 = keep([P, S // 16], U16, "lst3")
 
         def load_scales(engine, dram, plane):
-            for q in range(4):
+            for r in range(4):
                 engine.dma_start(
-                    out=plane[32 * q : 32 * q + 4, :].bitcast(I32).rearrange("r (a c) -> r a c", a=PASSES),
-                    in_=dram[:, 4 * q : 4 * q + 4, :].bitcast(I32).rearrange("a r c -> r a c"),
+                    out=plane[r:P:32, :].bitcast(I32).rearrange("q (a c) -> q a c", a=PASSES),
+                    in_=dram[:, r:16:4, :].bitcast(I32).rearrange("a q c -> q a c"),
                 )
 
         def load_packed_scales(engine, dram, plane):
@@ -68,16 +68,16 @@ def tile_list_star_conference_scores_kernel(
 
         w2_raw = keep([P, PASSES * H], U16, "w2_raw")
         tabw = [keep([P, T], U32, "tabw%d" % a) for a in range(PASSES)]
-        tab2w = keep([P, PASSES * T3], U32, "tab2w")
-        gain_sb = keep([P, PASSES, PACK], F32, "gain_sb")
+        tab2w = [keep([P, T3], U32, "tab2w%d" % a) for a in range(PASSES)]
+        gain_sb = keep([P, PASSES, 2 * PACK], F32, "gain_sb")
         ex_sb = keep([P, S2 // P], F32, "ex_sb")
         wgo_sb = keep([P, S], F32, "wgo_sb")
         page = [keep([P, T2], F32, "page%d" % c) for c in range(S2 // P)]
         w1_raw = {(a, b): keep([P, PACK, KP], F32, "w1_raw%d%d" % (a, b)) for a in range(PASSES) for b in range(PASSES)}
         season_sb = [keep([P, PACK, S], F32, "season%d" % b) for b in range(PASSES)]
 
-        def load_words(a):
-            nc.sync.dma_start(out=tabw[a][:].bitcast(I32), in_=tab_words[a].rearrange("p t i -> p (t i)").bitcast(I32))
+        def load_words(tile, words):
+            nc.sync.dma_start(out=tile[:].bitcast(I32), in_=words.rearrange("p t i -> p (t i)").bitcast(I32))
 
         def load_w1(a, b):
             nc.sync.dma_start(
@@ -85,33 +85,32 @@ def tile_list_star_conference_scores_kernel(
                 in_=w1[KP * a : KP * (a + 1), KP * b : KP * (b + 1)].rearrange("(p j) c -> p j c", j=PACK),
             )
 
-        def load_season(b):
+        def load_season(b, tp):
             rows = season[KP * b : KP * (b + 1), :].rearrange("(p t) j -> p t j", t=PACK)
-            for tp in range(2):
-                nc.sync.dma_start(out=season_sb[b][:, 2 * tp : 2 * tp + 2, :], in_=rows[:, 2 * tp : 2 * tp + 2, :])
+            nc.sync.dma_start(out=season_sb[b][:, 2 * tp : 2 * tp + 2, :], in_=rows[:, 2 * tp : 2 * tp + 2, :])
 
+        nc.sync.dma_start(out=gain_sb[:, :, :PACK], in_=gain.rearrange("(b p t) -> p b t", b=PASSES, t=PACK))
         nc.sync.dma_start(lst[:], offs)
         nc.sync.dma_start(
             out=w2_raw[:].bitcast(I32).rearrange("p (a c) -> p a c", a=PASSES),
             in_=w2_words.rearrange("a p c -> p a c").bitcast(I32),
         )
         load_scales(nc.sync, tab_scales, tabs)
-        load_words(0)
-        load_words(1)
+        load_words(tabw[0], tab_words[0])
+        load_words(tabw[1], tab_words[1])
         load_scales(nc.sync, w2_scales, w2s_raw)
         load_w1(0, 0)
-        nc.sync.dma_start(out=gain_sb[:], in_=gain.rearrange("(b p t) -> p b t", b=PASSES, t=PACK))
         load_w1(1, 0)
-        load_season(0)
+        load_season(0, 0)
+        load_season(0, 1)
         load_w1(0, 1)
         nc.sync.dma_start(lst2[:], offs2)
         load_packed_scales(nc.sync, tab2_scales, tab2s)
         load_w1(1, 1)
-        nc.sync.dma_start(
-            out=tab2w[:].bitcast(I32).rearrange("p (a c) -> p a c", a=PASSES),
-            in_=tab2_words.rearrange("a p t i -> p a (t i)").bitcast(I32),
-        )
-        load_season(1)
+        load_words(tab2w[0], tab2_words[0])
+        load_season(1, 0)
+        load_season(1, 1)
+        load_words(tab2w[1], tab2_words[1])
         nc.sync.dma_start(lst3[:], offs3)
         with nc.allow_non_contiguous_dma(reason="one value a partition"):
             nc.sync.dma_start(out=ex_sb[:], in_=ex.rearrange("(c p) -> p c", p=P))
@@ -262,7 +261,7 @@ def tile_list_star_conference_scores_kernel(
         v2s = keep([P, S2], U8, "v2s")
         nc.vector.tensor_copy(v2s[:], tab2s[:].indirect(lst2[:]))
         for a in range(PASSES):
-            nc.vector.tensor_copy(v2w[a][:], tab2w[:, T3 * a : T3 * (a + 1)].indirect(lst2[:]))
+            nc.vector.tensor_copy(v2w[a][:], tab2w[a][:].indirect(lst2[:]))
         h1 = [quantize_h(hb10, 1, 0, JH, nc.scalar.copy)]
         th11 = bend(1, w1q1, JH, JH)
         hb11 = join(1, th11, JH, JH)

@@ -1,6 +1,7 @@
 from contextlib import ExitStack
 
 import concourse.mybir as mybir
+from concourse.masks import make_identity
 
 K, H, T, S, T3, S2, T2 = 1024, 1024, 2048, 512, 1024, 512, 1024
 FLOPS = 2 * S * (2 * K * H + S2 * H + S2 * K)
@@ -22,8 +23,8 @@ P = 128
 PACK = 4
 KP = P * PACK
 PASSES = 2
-JH = S // 2
-REUSES = {"v2w0": "grouped11", "v2w1": "th1_0_2", "hw0_0": "bent1_0_0", "bent1_256_0": "hi1_0", "bent1_256_2": "hb1_0", "hi0_0": "w1_raw11"}
+HALF = S // 2
+ROW_TILES = S2 // P
 SCALAR_SHARE = {(0, 0): 64, (1, 0): 48, (0, 1): 128, (1, 1): 64}
 
 
@@ -34,28 +35,28 @@ def tile_list_star_conference_scores_kernel(
     nc = tc.nc
     with ExitStack() as ctx:
         held = ctx.enter_context(tc.tile_pool(name="held", bufs=1))
-        ring = ctx.enter_context(tc.tile_pool(name="ring", bufs=8))
+        ring = ctx.enter_context(tc.tile_pool(name="ring", bufs=3))
         psum = ctx.enter_context(tc.psum_pool(name="psum", bufs=4))
 
-        def keep(shape, dtype, name):
-            return held.tile(shape, dtype, name=name, tag=REUSES.get(name, name), align_bytes=64)
+        def keep(shape, dtype, name, after=None):
+            return held.tile(shape, dtype, name=name, tag=after or name, align_bytes=64)
 
         lst = keep([P, S // 16], U16, "lst")
         lst2 = keep([P, S2 // 16], U16, "lst2")
         lst3 = keep([P, S // 16], U16, "lst3")
 
-        def load_scales(engine, dram, plane):
-            for r in range(4):
-                engine.dma_start(
-                    out=plane[r:P:32, :].bitcast(I32).rearrange("q (a c) -> q a c", a=PASSES),
-                    in_=dram[:, r:16:4, :].bitcast(I32).rearrange("a q c -> q a c"),
+        def load_planes_side_by_side(dram, planes):
+            for r in range(PACK):
+                nc.sync.dma_start(
+                    out=planes[r:P:32, :].bitcast(I32).rearrange("q (a c) -> q a c", a=PASSES),
+                    in_=dram[:, r:16:PACK, :].bitcast(I32).rearrange("a q c -> q a c"),
                 )
 
-        def load_packed_scales(engine, dram, plane):
-            for q in range(4):
-                engine.dma_start(
-                    out=plane[32 * q : 32 * q + 8, :].bitcast(I32),
-                    in_=dram[:, 4 * q : 4 * q + 4, :].bitcast(I32),
+        def load_planes_stacked(dram, planes):
+            for q in range(P // 32):
+                nc.sync.dma_start(
+                    out=planes[32 * q : 32 * q + PASSES * PACK, :].bitcast(I32),
+                    in_=dram[:, PACK * q : PACK * (q + 1), :].bitcast(I32),
                 )
 
         tabs = keep([P, PASSES * T], U8, "tabs")
@@ -70,9 +71,9 @@ def tile_list_star_conference_scores_kernel(
         tabw = [keep([P, T], U32, "tabw%d" % a) for a in range(PASSES)]
         tab2w = [keep([P, T3], U32, "tab2w%d" % a) for a in range(PASSES)]
         gain_sb = keep([P, PASSES, 2 * PACK], F32, "gain_sb")
-        ex_sb = keep([P, S2 // P], F32, "ex_sb")
+        ex_sb = keep([P, ROW_TILES], F32, "ex_sb")
         wgo_sb = keep([P, S], F32, "wgo_sb")
-        page = [keep([P, T2], F32, "page%d" % c) for c in range(S2 // P)]
+        page = [keep([P, T2], F32, "page%d" % c) for c in range(ROW_TILES)]
         w1_raw = {(a, b): keep([P, PACK, KP], F32, "w1_raw%d%d" % (a, b)) for a in range(PASSES) for b in range(PASSES)}
         season_sb = [keep([P, PACK, S], F32, "season%d" % b) for b in range(PASSES)]
 
@@ -82,12 +83,13 @@ def tile_list_star_conference_scores_kernel(
         def load_w1(a, b):
             nc.sync.dma_start(
                 out=w1_raw[a, b][:],
-                in_=w1[KP * a : KP * (a + 1), KP * b : KP * (b + 1)].rearrange("(p j) c -> p j c", j=PACK),
+                in_=w1[KP * a : KP * (a + 1), KP * b : KP * (b + 1)].rearrange("(p i) c -> p i c", i=PACK),
             )
 
-        def load_season(b, tp):
+        def load_season(b, pair):
             rows = season[KP * b : KP * (b + 1), :].rearrange("(p t) j -> p t j", t=PACK)
-            nc.sync.dma_start(out=season_sb[b][:, 2 * tp : 2 * tp + 2, :], in_=rows[:, 2 * tp : 2 * tp + 2, :])
+            ts = slice(2 * pair, 2 * pair + 2)
+            nc.sync.dma_start(out=season_sb[b][:, ts, :], in_=rows[:, ts, :])
 
         nc.sync.dma_start(out=gain_sb[:, :, :PACK], in_=gain.rearrange("(b p t) -> p b t", b=PASSES, t=PACK))
         nc.sync.dma_start(lst[:], offs)
@@ -95,34 +97,37 @@ def tile_list_star_conference_scores_kernel(
             out=w2_raw[:].bitcast(I32).rearrange("p (a c) -> p a c", a=PASSES),
             in_=w2_words.rearrange("a p c -> p a c").bitcast(I32),
         )
-        load_scales(nc.sync, tab_scales, tabs)
+        load_planes_side_by_side(tab_scales, tabs)
         load_words(tabw[0], tab_words[0])
         load_words(tabw[1], tab_words[1])
-        load_scales(nc.sync, w2_scales, w2s_raw)
+        load_planes_side_by_side(w2_scales, w2s_raw)
         load_w1(0, 0)
         load_w1(1, 0)
         load_season(0, 0)
         load_season(0, 1)
         load_w1(0, 1)
         nc.sync.dma_start(lst2[:], offs2)
-        load_packed_scales(nc.sync, tab2_scales, tab2s)
+        load_planes_stacked(tab2_scales, tab2s)
         load_w1(1, 1)
         load_words(tab2w[0], tab2_words[0])
         load_season(1, 0)
         load_season(1, 1)
         load_words(tab2w[1], tab2_words[1])
         nc.sync.dma_start(lst3[:], offs3)
-        with nc.allow_non_contiguous_dma(reason="one value a partition"):
+        with nc.allow_non_contiguous_dma(reason="ex[128 c + p] at [p, c]: one value a partition and row tile"):
             nc.sync.dma_start(out=ex_sb[:], in_=ex.rearrange("(c p) -> p c", p=P))
         nc.sync.dma_start(out=wgo_sb[:], in_=wgo)
-        for c in range(S2 // P):
+        for c in range(ROW_TILES):
             nc.sync.dma_start(out=page[c][:], in_=page1[P * c : P * (c + 1), :])
 
+        def deal_columns(dealt, raw):
+            nc.vector.tensor_copy(
+                out=dealt[:].rearrange("p (g t m) -> p g t m", t=PACK, m=P),
+                in_=raw[:].rearrange("p (g m t) -> p g t m", t=PACK, m=P),
+            )
+
         w2w = keep([P, PASSES * H], U16, "w2w")
-        nc.vector.tensor_copy(
-            out=w2w[:].rearrange("p (g t m) -> p g t m", t=PACK, m=P),
-            in_=w2_raw[:].rearrange("p (g m t) -> p g t m", t=PACK, m=P),
-        )
+        deal_columns(w2w, w2_raw)
         vs = keep([P, PASSES, S], U8, "vs")
         for a in range(PASSES):
             nc.vector.tensor_copy(vs[:, a, :], tabs[:, T * a : T * (a + 1)].indirect(lst[:]))
@@ -130,48 +135,55 @@ def tile_list_star_conference_scores_kernel(
         for a in range(PASSES):
             nc.vector.tensor_copy(vw[a][:], tabw[a][:].indirect(lst[:]))
         w2s = keep([P, PASSES * H], U8, "w2s")
-        nc.vector.tensor_copy(
-            out=w2s[:].rearrange("p (g t m) -> p g t m", t=PACK, m=P),
-            in_=w2s_raw[:].rearrange("p (g m t) -> p g t m", t=PACK, m=P),
-        )
-
+        deal_columns(w2s, w2s_raw)
 
         def quantize_w1(a, b):
             grouped = keep([P, PACK, P, PACK], BF16, "grouped%d%d" % (a, b))
-            dst = grouped[:].rearrange("p t m j -> p m j t")
-            src = w1_raw[a, b][:].rearrange("p j (m t) -> p m j t", t=PACK)
+            dst = grouped[:].rearrange("p t m i -> p m i t")
+            src = w1_raw[a, b][:].rearrange("p i (m t) -> p m i t", t=PACK)
             cut = SCALAR_SHARE[a, b]
-            if cut > 0:
-                nc.scalar.copy(out=dst[:, :cut], in_=src[:, :cut])
+            nc.scalar.copy(out=dst[:, :cut], in_=src[:, :cut])
             if cut < P:
                 nc.vector.tensor_copy(out=dst[:, cut:], in_=src[:, cut:])
             words = keep([P, KP], U32, "w1w%d%d" % (a, b))
             scales = keep([P, KP], U8, "w1s%d%d" % (a, b))
-            parts = 1 + a
-            for i in range(parts):
-                ts = slice(PACK // parts * i, PACK // parts * (i + 1))
-                cols = slice(KP // parts * i, KP // parts * (i + 1))
+            parts = 2 if a == PASSES - 1 else 1
+            for part in range(parts):
+                ts = slice(PACK // parts * part, PACK // parts * (part + 1))
+                cols = slice(KP // parts * part, KP // parts * (part + 1))
                 nc.vector.quantize_mx(
                     out=words[:, cols].bitcast(FP8X4), scales=scales[:, cols],
-                    in_=grouped[:, ts].rearrange("p t m j -> p (t m j)"),
+                    in_=grouped[:, ts].rearrange("p t m i -> p (t m i)"),
                 )
             return words, scales
 
-        def bend(b, w1q, j0, nj):
+        def product(bank, stationary, moving):
+            ranges = bank.shape[1]
+            for a in range(PASSES):
+                for u in range(ranges):
+                    lhs, lhs_scale = stationary(a, u)
+                    rhs, rhs_scale = moving(a)
+                    nc.tensor.matmul_mx(
+                        out=bank[:, u, :], lhsT=lhs, lhsT_scale=lhs_scale, rhs=rhs, rhs_scale=rhs_scale,
+                        start=(a == 0 and u == 0), stop=(a == PASSES - 1 and u == ranges - 1),
+                    )
+
+        def visits(jc):
+            return lambda a: (vw[a][:, jc].bitcast(FP8X4), vs[:, a, jc])
+
+        def bend(b, w1q, j0, nj, after=None):
             jc = slice(j0, j0 + nj)
             nt = S // nj
             tanhs = []
             for t0 in range(0, PACK, nt):
+
+                def w1_columns(a, u):
+                    cols = slice(P * (t0 + u), P * (t0 + u + 1))
+                    return w1q[a][0][:, cols].bitcast(FP8X4), w1q[a][1][:, cols]
+
                 b1 = psum.tile([P, nt, nj], F32, name="acc1")
-                for a in range(PASSES):
-                    for u in range(nt):
-                        cols = slice(P * (t0 + u), P * (t0 + u + 1))
-                        nc.tensor.matmul_mx(
-                            out=b1[:, u, :], lhsT=w1q[a][0][:, cols].bitcast(FP8X4), lhsT_scale=w1q[a][1][:, cols],
-                            rhs=vw[a][:, jc].bitcast(FP8X4), rhs_scale=vs[:, a, jc],
-                            start=(a == 0 and u == 0), stop=(a == PASSES - 1 and u == nt - 1),
-                        )
-                bent = keep([P, nt, nj], F32, "bent%d_%d_%d" % (b, j0, t0))
+                product(b1, w1_columns, visits(jc))
+                bent = keep([P, nt, nj], F32, "bent%d_%d_%d" % (b, j0, t0), after[t0 // nt] if after else None)
                 nc.vector.tensor_tensor(bent[:], b1[:], season_sb[b][:, t0 : t0 + nt, jc], MULT)
                 th = keep([P, nt, nj], F32, "th%d_%d_%d" % (b, j0, t0))
                 nc.scalar.activation(th[:], bent[:], TANH)
@@ -183,15 +195,13 @@ def tile_list_star_conference_scores_kernel(
             nt = S // nj
             hb = keep([P, PACK, nj], BF16, "hb%d_%d" % (b, j0))
             for t0 in range(0, PACK, nt):
+
+                def w2_columns(a, u):
+                    c0 = H * a + KP * b + P * (t0 + u)
+                    return w2w[:, c0 : c0 + P].bitcast(FP4X4), w2s[:, c0 : c0 + P]
+
                 b2 = psum.tile([P, nt, nj], F32, name="acc2")
-                for a in range(PASSES):
-                    for u in range(nt):
-                        c0 = H * a + KP * b + P * (t0 + u)
-                        nc.tensor.matmul_mx(
-                            out=b2[:, u, :], lhsT=w2w[:, c0 : c0 + P].bitcast(FP4X4), lhsT_scale=w2s[:, c0 : c0 + P],
-                            rhs=vw[a][:, jc].bitcast(FP8X4), rhs_scale=vs[:, a, jc],
-                            start=(a == 0 and u == 0), stop=(a == PASSES - 1 and u == nt - 1),
-                        )
+                product(b2, w2_columns, visits(jc))
                 for u in range(nt):
                     t = t0 + u
                     nc.vector.scalar_tensor_tensor(
@@ -199,72 +209,90 @@ def tile_list_star_conference_scores_kernel(
                     )
             return hb
 
-        def quantize_h(hb, b, j0, nj, weave):
-            hi = keep([P, nj, PACK], BF16, "hi%d_%d" % (b, j0))
-            dst = hi[:].rearrange("p (c i) t -> p c t i", i=4)
+        def quantize_h(hb, b, j0, nj, copy, after=None):
+            woven = keep([P, nj, PACK], BF16, "woven%d_%d" % (b, j0), after)
+            dst = woven[:].rearrange("p (c i) t -> p c t i", i=4)
             src = hb[:].rearrange("p t (c i) -> p c t i", i=4)
-            for c0 in range(0, nj // 4, JH // 4):
-                weave(dst[:, c0 : c0 + JH // 4], src[:, c0 : c0 + JH // 4])
+            for c0 in range(0, nj // 4, HALF // 4):
+                copy(dst[:, c0 : c0 + HALF // 4], src[:, c0 : c0 + HALF // 4])
             words = keep([P, nj], U32, "hw%d_%d" % (b, j0))
             scales = keep([P, nj], U8, "hs%d_%d" % (b, j0))
             nc.vector.quantize_mx(
-                out=words[:].bitcast(FP8X4), scales=scales[:], in_=hi[:].rearrange("p j t -> p (j t)")
+                out=words[:].bitcast(FP8X4), scales=scales[:], in_=woven[:].rearrange("p j t -> p (j t)")
             )
             return words, scales
 
-        def score(jh, h1q):
-            hq = [(h0_words[:, JH * jh : JH * (jh + 1)], h0_scales[:, JH * jh : JH * (jh + 1)]), (h1q[0][:], h1q[1][:])]
-            jc = slice(JH * jh, JH * (jh + 1))
-            for cp in range(2):
-                e = psum.tile([P, 2, JH], F32, name="acc1")
-                for b in range(PASSES):
-                    for u in range(2):
-                        cols = slice(P * (2 * cp + u), P * (2 * cp + u + 1))
-                        nc.tensor.matmul_mx(
-                            out=e[:, u, :], lhsT=v2w[b][:, cols].bitcast(FP8X4), lhsT_scale=v2s[4 * b :, cols],
-                            rhs=hq[b][0].bitcast(FP8X4), rhs_scale=hq[b][1],
-                            start=(b == 0 and u == 0), stop=(b == PASSES - 1 and u == 1),
-                        )
-                d = psum.tile([P, 2, JH], F32, name="acc2")
-                for a in range(PASSES):
-                    for u in range(2):
-                        cols = slice(P * (2 * cp + u), P * (2 * cp + u + 1))
-                        nc.tensor.matmul_mx(
-                            out=d[:, u, :], lhsT=v2w[a][:, cols].bitcast(FP8X4), lhsT_scale=v2s[4 * a :, cols],
-                            rhs=vw[a][:, jc].bitcast(FP8X4), rhs_scale=vs[:, a, jc],
-                            start=(a == 0 and u == 0), stop=(a == PASSES - 1 and u == 1),
-                        )
-                scaled = ring.tile([P, 2, JH], F32, name="scaled")
-                for u in range(2):
-                    c = 2 * cp + u
-                    nc.scalar.activation(scaled[:, u, :], e[:, u, :], COPY, scale=ex_sb[:, c : c + 1])
-                z = ring.tile([P, 2, JH], F32, name="z")
-                nc.vector.tensor_tensor(z[:], scaled[:], d[:], ADD)
-                for u in range(2):
-                    c = 2 * cp + u
-                    y = ring.tile([P, JH], F32, name="y", bufs=4)
-                    nc.scalar.activation(y[:], z[:, u, :], TANH)
-                    nc.vector.tensor_tensor(
-                        page[c][:].indirect(lst3[:, (JH // 16) * jh : (JH // 16) * (jh + 1)]), y[:], wgo_sb[:, jc], MULT
+        ident = keep([P, P], F32, "ident")
+        make_identity(nc, ident[:])
+
+        def sum_on_vector(scaled, d):
+            z = ring.tile([P, 2, HALF], F32, name="z")
+            nc.vector.tensor_tensor(z[:], scaled[:], d[:], ADD)
+            return z
+
+        def sum_by_transposes(scaled, d):
+            d_sb = ring.tile([P, 2, HALF], F32, name="d_sb")
+            nc.scalar.copy(out=d_sb[:], in_=d[:])
+            squares = [(u, x) for u in range(2) for x in range(HALF // P)]
+            turned = psum.tile([P, 2, HALF // P, P], F32, name="acc1")
+            for term in (d_sb, scaled):
+                for u, x in squares:
+                    nc.tensor.matmul(
+                        turned[:, u, x, :], term[:, u, P * x : P * (x + 1)], ident[:], is_transpose=True,
+                        start=(term is d_sb and (u, x) == squares[0]),
+                        stop=(term is scaled and (u, x) == squares[-1]),
                     )
-                    if jh == 1:
+            turned_sb = ring.tile([P, 2, HALF // P, P], F32, name="turned_sb")
+            nc.scalar.copy(out=turned_sb[:], in_=turned[:])
+            z = psum.tile([P, 2, HALF], F32, name="acc2")
+            for u, x in squares:
+                nc.tensor.transpose(z[:, u, P * x : P * (x + 1)], turned_sb[:, u, x, :], ident[:])
+            return z
+
+        def score(half, h_block0, h_block1, add):
+            jc = slice(HALF * half, HALF * (half + 1))
+            h_passes = [
+                (h_block0[0][:, jc].bitcast(FP8X4), h_block0[1][:, jc]),
+                (h_block1[0][:].bitcast(FP8X4), h_block1[1][:]),
+            ]
+            for c0 in range(0, ROW_TILES, 2):
+
+                def exemplars(a, u):
+                    cols = slice(P * (c0 + u), P * (c0 + u + 1))
+                    return v2w[a][:, cols].bitcast(FP8X4), v2s[PACK * a :, cols]
+
+                e = psum.tile([P, 2, HALF], F32, name="acc1")
+                product(e, exemplars, lambda b: h_passes[b])
+                d = psum.tile([P, 2, HALF], F32, name="acc2")
+                product(d, exemplars, visits(jc))
+                scaled = ring.tile([P, 2, HALF], F32, name="scaled")
+                for u in range(2):
+                    nc.scalar.activation(scaled[:, u, :], e[:, u, :], COPY, scale=ex_sb[:, c0 + u : c0 + u + 1])
+                z = add(scaled, d)
+                for u in range(2):
+                    c = c0 + u
+                    y = ring.tile([P, HALF], F32, name="y", bufs=ROW_TILES)
+                    nc.scalar.activation(y[:], z[:, u, :], TANH)
+                    places = lst3[:, (HALF // 16) * half : (HALF // 16) * (half + 1)]
+                    nc.vector.tensor_tensor(page[c][:].indirect(places), y[:], wgo_sb[:, jc], MULT)
+                    if half == 1:
                         nc.sync.dma_start(out=out[P * c : P * (c + 1), :], in_=page[c][:])
 
         w1q0 = [quantize_w1(a, 0) for a in range(PASSES)]
         th0 = bend(0, w1q0, 0, S)
         w1q1 = [quantize_w1(a, 1) for a in range(PASSES)]
         hb0 = join(0, th0, 0, S)
-        th10 = bend(1, w1q1, 0, JH)
-        hb10 = join(1, th10, 0, JH)
-        h0_words, h0_scales = quantize_h(hb0, 0, 0, S, nc.scalar.copy)
-        v2w = [keep([P, S2], U32, "v2w%d" % a) for a in range(PASSES)]
+        th10 = bend(1, w1q1, 0, HALF)
+        hb10 = join(1, th10, 0, HALF)
+        h0 = quantize_h(hb0, 0, 0, S, nc.scalar.copy, after="w1_raw11")
+        v2w = [keep([P, S2], U32, "v2w0"), keep([P, S2], U32, "v2w1", after="th1_0_2")]
         v2s = keep([P, S2], U8, "v2s")
         nc.vector.tensor_copy(v2s[:], tab2s[:].indirect(lst2[:]))
         for a in range(PASSES):
             nc.vector.tensor_copy(v2w[a][:], tab2w[a][:].indirect(lst2[:]))
-        h1 = [quantize_h(hb10, 1, 0, JH, nc.scalar.copy)]
-        th11 = bend(1, w1q1, JH, JH)
-        hb11 = join(1, th11, JH, JH)
-        h1.append(quantize_h(hb11, 1, JH, JH, nc.scalar.copy))
-        score(0, h1[0])
-        score(1, h1[1])
+        h10 = quantize_h(hb10, 1, 0, HALF, nc.scalar.copy)
+        th11 = bend(1, w1q1, HALF, HALF, after=("hb1_0", "woven1_0"))
+        hb11 = join(1, th11, HALF, HALF)
+        h11 = quantize_h(hb11, 1, HALF, HALF, nc.vector.tensor_copy)
+        score(0, h0, h10, sum_on_vector)
+        score(1, h0, h11, sum_by_transposes)

from contextlib import ExitStack

import concourse.mybir as mybir
from concourse.masks import make_identity

K, H, T, S, T3, S2, T2 = 1024, 1024, 2048, 512, 1024, 512, 1024
FLOPS = 2 * S * (2 * K * H + S2 * H + S2 * K)

F32 = mybir.dt.float32
BF16 = mybir.dt.bfloat16
I32 = mybir.dt.int32
U32 = mybir.dt.uint32
U16 = mybir.dt.uint16
U8 = mybir.dt.uint8
FP8X4 = mybir.dt.float8_e4m3fn_x4
FP4X4 = mybir.dt.float4_e2m1fn_x4
MULT = mybir.AluOpType.mult
ADD = mybir.AluOpType.add
COPY = mybir.ActivationFunctionType.Copy
TANH = mybir.ActivationFunctionType.Tanh

P = 128
PACK = 4
KP = P * PACK
PASSES = 2
HALF = S // 2
ROW_TILES = S2 // P
SCALAR_SHARE = {(0, 0): 64, (1, 0): 48, (0, 1): 128, (1, 1): 64}


def tile_list_star_conference_scores_kernel(
    tc, tab_words, tab_scales, tab2_words, tab2_scales, offs, offs2, offs3,
    w1, w2_words, w2_scales, season, gain, ex, page1, wgo, out,
):
    nc = tc.nc
    with ExitStack() as ctx:
        held = ctx.enter_context(tc.tile_pool(name="held", bufs=1))
        ring = ctx.enter_context(tc.tile_pool(name="ring", bufs=3))
        psum = ctx.enter_context(tc.psum_pool(name="psum", bufs=4))

        def keep(shape, dtype, name, after=None):
            return held.tile(shape, dtype, name=name, tag=after or name, align_bytes=64)

        lst = keep([P, S // 16], U16, "lst")
        lst2 = keep([P, S2 // 16], U16, "lst2")
        lst3 = keep([P, S // 16], U16, "lst3")

        def load_planes_side_by_side(dram, planes):
            for r in range(PACK):
                nc.sync.dma_start(
                    out=planes[r:P:32, :].bitcast(I32).rearrange("q (a c) -> q a c", a=PASSES),
                    in_=dram[:, r:16:PACK, :].bitcast(I32).rearrange("a q c -> q a c"),
                )

        def load_planes_stacked(dram, planes):
            for q in range(P // 32):
                nc.sync.dma_start(
                    out=planes[32 * q : 32 * q + PASSES * PACK, :].bitcast(I32),
                    in_=dram[:, PACK * q : PACK * (q + 1), :].bitcast(I32),
                )

        tabs = keep([P, PASSES * T], U8, "tabs")
        w2s_raw = keep([P, PASSES * H], U8, "w2s_raw")
        tab2s = keep([P, T3], U8, "tab2s")
        nc.gpsimd.memset(tabs[:, :T].bitcast(I32), 0)
        nc.vector.memset(tabs[:, T:].bitcast(I32), 0)
        nc.vector.memset(w2s_raw[:].bitcast(I32), 0)
        nc.gpsimd.memset(tab2s[:].bitcast(I32), 0)

        w2_raw = keep([P, PASSES * H], U16, "w2_raw")
        tabw = [keep([P, T], U32, "tabw%d" % a) for a in range(PASSES)]
        tab2w = [keep([P, T3], U32, "tab2w%d" % a) for a in range(PASSES)]
        gain_sb = keep([P, PASSES, 2 * PACK], F32, "gain_sb")
        ex_sb = keep([P, ROW_TILES], F32, "ex_sb")
        wgo_sb = keep([P, S], F32, "wgo_sb")
        page = [keep([P, T2], F32, "page%d" % c) for c in range(ROW_TILES)]
        w1_raw = {(a, b): keep([P, PACK, KP], F32, "w1_raw%d%d" % (a, b)) for a in range(PASSES) for b in range(PASSES)}
        season_sb = [keep([P, PACK, S], F32, "season%d" % b) for b in range(PASSES)]

        def load_words(tile, words):
            nc.sync.dma_start(out=tile[:].bitcast(I32), in_=words.rearrange("p t i -> p (t i)").bitcast(I32))

        def load_w1(a, b):
            nc.sync.dma_start(
                out=w1_raw[a, b][:],
                in_=w1[KP * a : KP * (a + 1), KP * b : KP * (b + 1)].rearrange("(p i) c -> p i c", i=PACK),
            )

        def load_season(b, pair):
            rows = season[KP * b : KP * (b + 1), :].rearrange("(p t) j -> p t j", t=PACK)
            ts = slice(2 * pair, 2 * pair + 2)
            nc.sync.dma_start(out=season_sb[b][:, ts, :], in_=rows[:, ts, :])

        nc.sync.dma_start(out=gain_sb[:, :, :PACK], in_=gain.rearrange("(b p t) -> p b t", b=PASSES, t=PACK))
        nc.sync.dma_start(lst[:], offs)
        nc.sync.dma_start(
            out=w2_raw[:].bitcast(I32).rearrange("p (a c) -> p a c", a=PASSES),
            in_=w2_words.rearrange("a p c -> p a c").bitcast(I32),
        )
        load_planes_side_by_side(tab_scales, tabs)
        load_words(tabw[0], tab_words[0])
        load_words(tabw[1], tab_words[1])
        load_planes_side_by_side(w2_scales, w2s_raw)
        load_w1(0, 0)
        load_w1(1, 0)
        load_season(0, 0)
        load_season(0, 1)
        load_w1(0, 1)
        nc.sync.dma_start(lst2[:], offs2)
        load_planes_stacked(tab2_scales, tab2s)
        load_w1(1, 1)
        load_words(tab2w[0], tab2_words[0])
        load_season(1, 0)
        load_season(1, 1)
        load_words(tab2w[1], tab2_words[1])
        nc.sync.dma_start(lst3[:], offs3)
        with nc.allow_non_contiguous_dma(reason="ex[128 c + p] at [p, c]: one value a partition and row tile"):
            nc.sync.dma_start(out=ex_sb[:], in_=ex.rearrange("(c p) -> p c", p=P))
        nc.sync.dma_start(out=wgo_sb[:], in_=wgo)
        for c in range(ROW_TILES):
            nc.sync.dma_start(out=page[c][:], in_=page1[P * c : P * (c + 1), :])

        def deal_columns(dealt, raw):
            nc.vector.tensor_copy(
                out=dealt[:].rearrange("p (g t m) -> p g t m", t=PACK, m=P),
                in_=raw[:].rearrange("p (g m t) -> p g t m", t=PACK, m=P),
            )

        w2w = keep([P, PASSES * H], U16, "w2w")
        deal_columns(w2w, w2_raw)
        vs = keep([P, PASSES, S], U8, "vs")
        for a in range(PASSES):
            nc.vector.tensor_copy(vs[:, a, :], tabs[:, T * a : T * (a + 1)].indirect(lst[:]))
        vw = [keep([P, S], U32, "vw%d" % a) for a in range(PASSES)]
        for a in range(PASSES):
            nc.vector.tensor_copy(vw[a][:], tabw[a][:].indirect(lst[:]))
        w2s = keep([P, PASSES * H], U8, "w2s")
        deal_columns(w2s, w2s_raw)

        def quantize_w1(a, b):
            grouped = keep([P, PACK, P, PACK], BF16, "grouped%d%d" % (a, b))
            dst = grouped[:].rearrange("p t m i -> p m i t")
            src = w1_raw[a, b][:].rearrange("p i (m t) -> p m i t", t=PACK)
            cut = SCALAR_SHARE[a, b]
            nc.scalar.copy(out=dst[:, :cut], in_=src[:, :cut])
            if cut < P:
                nc.vector.tensor_copy(out=dst[:, cut:], in_=src[:, cut:])
            words = keep([P, KP], U32, "w1w%d%d" % (a, b))
            scales = keep([P, KP], U8, "w1s%d%d" % (a, b))
            parts = 2 if a == PASSES - 1 else 1
            for part in range(parts):
                ts = slice(PACK // parts * part, PACK // parts * (part + 1))
                cols = slice(KP // parts * part, KP // parts * (part + 1))
                nc.vector.quantize_mx(
                    out=words[:, cols].bitcast(FP8X4), scales=scales[:, cols],
                    in_=grouped[:, ts].rearrange("p t m i -> p (t m i)"),
                )
            return words, scales

        def product(bank, stationary, moving):
            ranges = bank.shape[1]
            for a in range(PASSES):
                for u in range(ranges):
                    lhs, lhs_scale = stationary(a, u)
                    rhs, rhs_scale = moving(a)
                    nc.tensor.matmul_mx(
                        out=bank[:, u, :], lhsT=lhs, lhsT_scale=lhs_scale, rhs=rhs, rhs_scale=rhs_scale,
                        start=(a == 0 and u == 0), stop=(a == PASSES - 1 and u == ranges - 1),
                    )

        def visits(jc):
            return lambda a: (vw[a][:, jc].bitcast(FP8X4), vs[:, a, jc])

        def bend(b, w1q, j0, nj, after=None):
            jc = slice(j0, j0 + nj)
            nt = S // nj
            tanhs = []
            for t0 in range(0, PACK, nt):

                def w1_columns(a, u):
                    cols = slice(P * (t0 + u), P * (t0 + u + 1))
                    return w1q[a][0][:, cols].bitcast(FP8X4), w1q[a][1][:, cols]

                b1 = psum.tile([P, nt, nj], F32, name="acc1")
                product(b1, w1_columns, visits(jc))
                bent = keep([P, nt, nj], F32, "bent%d_%d_%d" % (b, j0, t0), after[t0 // nt] if after else None)
                nc.vector.tensor_tensor(bent[:], b1[:], season_sb[b][:, t0 : t0 + nt, jc], MULT)
                th = keep([P, nt, nj], F32, "th%d_%d_%d" % (b, j0, t0))
                nc.scalar.activation(th[:], bent[:], TANH)
                tanhs.append(th)
            return tanhs

        def join(b, tanhs, j0, nj):
            jc = slice(j0, j0 + nj)
            nt = S // nj
            hb = keep([P, PACK, nj], BF16, "hb%d_%d" % (b, j0))
            for t0 in range(0, PACK, nt):

                def w2_columns(a, u):
                    c0 = H * a + KP * b + P * (t0 + u)
                    return w2w[:, c0 : c0 + P].bitcast(FP4X4), w2s[:, c0 : c0 + P]

                b2 = psum.tile([P, nt, nj], F32, name="acc2")
                product(b2, w2_columns, visits(jc))
                for u in range(nt):
                    t = t0 + u
                    nc.vector.scalar_tensor_tensor(
                        hb[:, t, :], tanhs[t0 // nt][:, u, :], gain_sb[:, b, t : t + 1], b2[:, u, :], MULT, ADD
                    )
            return hb

        def quantize_h(hb, b, j0, nj, copy, after=None):
            woven = keep([P, nj, PACK], BF16, "woven%d_%d" % (b, j0), after)
            dst = woven[:].rearrange("p (c i) t -> p c t i", i=4)
            src = hb[:].rearrange("p t (c i) -> p c t i", i=4)
            for c0 in range(0, nj // 4, HALF // 4):
                copy(dst[:, c0 : c0 + HALF // 4], src[:, c0 : c0 + HALF // 4])
            words = keep([P, nj], U32, "hw%d_%d" % (b, j0))
            scales = keep([P, nj], U8, "hs%d_%d" % (b, j0))
            nc.vector.quantize_mx(
                out=words[:].bitcast(FP8X4), scales=scales[:], in_=woven[:].rearrange("p j t -> p (j t)")
            )
            return words, scales

        ident = keep([P, P], F32, "ident")
        make_identity(nc, ident[:])

        def sum_on_vector(scaled, d):
            z = ring.tile([P, 2, HALF], F32, name="z")
            nc.vector.tensor_tensor(z[:], scaled[:], d[:], ADD)
            return z

        def sum_by_transposes(scaled, d):
            d_sb = ring.tile([P, 2, HALF], F32, name="d_sb")
            nc.scalar.copy(out=d_sb[:], in_=d[:])
            squares = [(u, x) for u in range(2) for x in range(HALF // P)]
            turned = psum.tile([P, 2, HALF // P, P], F32, name="acc1")
            for term in (d_sb, scaled):
                for u, x in squares:
                    nc.tensor.matmul(
                        turned[:, u, x, :], term[:, u, P * x : P * (x + 1)], ident[:], is_transpose=True,
                        start=(term is d_sb and (u, x) == squares[0]),
                        stop=(term is scaled and (u, x) == squares[-1]),
                    )
            turned_sb = ring.tile([P, 2, HALF // P, P], F32, name="turned_sb")
            nc.scalar.copy(out=turned_sb[:], in_=turned[:])
            z = psum.tile([P, 2, HALF], F32, name="acc2")
            for u, x in squares:
                nc.tensor.transpose(z[:, u, P * x : P * (x + 1)], turned_sb[:, u, x, :], ident[:])
            return z

        def score(half, h_block0, h_block1, add):
            jc = slice(HALF * half, HALF * (half + 1))
            h_passes = [
                (h_block0[0][:, jc].bitcast(FP8X4), h_block0[1][:, jc]),
                (h_block1[0][:].bitcast(FP8X4), h_block1[1][:]),
            ]
            for c0 in range(0, ROW_TILES, 2):

                def exemplars(a, u):
                    cols = slice(P * (c0 + u), P * (c0 + u + 1))
                    return v2w[a][:, cols].bitcast(FP8X4), v2s[PACK * a :, cols]

                e = psum.tile([P, 2, HALF], F32, name="acc1")
                product(e, exemplars, lambda b: h_passes[b])
                d = psum.tile([P, 2, HALF], F32, name="acc2")
                product(d, exemplars, visits(jc))
                scaled = ring.tile([P, 2, HALF], F32, name="scaled")
                for u in range(2):
                    nc.scalar.activation(scaled[:, u, :], e[:, u, :], COPY, scale=ex_sb[:, c0 + u : c0 + u + 1])
                z = add(scaled, d)
                for u in range(2):
                    c = c0 + u
                    y = ring.tile([P, HALF], F32, name="y", bufs=ROW_TILES)
                    nc.scalar.activation(y[:], z[:, u, :], TANH)
                    places = lst3[:, (HALF // 16) * half : (HALF // 16) * (half + 1)]
                    nc.vector.tensor_tensor(page[c][:].indirect(places), y[:], wgo_sb[:, jc], MULT)
                    if half == 1:
                        nc.sync.dma_start(out=out[P * c : P * (c + 1), :], in_=page[c][:])

        w1q0 = [quantize_w1(a, 0) for a in range(PASSES)]
        th0 = bend(0, w1q0, 0, S)
        w1q1 = [quantize_w1(a, 1) for a in range(PASSES)]
        hb0 = join(0, th0, 0, S)
        th10 = bend(1, w1q1, 0, HALF)
        hb10 = join(1, th10, 0, HALF)
        h0 = quantize_h(hb0, 0, 0, S, nc.scalar.copy, after="w1_raw11")
        v2w = [keep([P, S2], U32, "v2w0"), keep([P, S2], U32, "v2w1", after="th1_0_2")]
        v2s = keep([P, S2], U8, "v2s")
        nc.vector.tensor_copy(v2s[:], tab2s[:].indirect(lst2[:]))
        for a in range(PASSES):
            nc.vector.tensor_copy(v2w[a][:], tab2w[a][:].indirect(lst2[:]))
        h10 = quantize_h(hb10, 1, 0, HALF, nc.scalar.copy)
        th11 = bend(1, w1q1, HALF, HALF, after=("hb1_0", "woven1_0"))
        hb11 = join(1, th11, HALF, HALF)
        h11 = quantize_h(hb11, 1, HALF, HALF, nc.vector.tensor_copy)
        score(0, h0, h10, sum_on_vector)
        score(1, h0, h11, sum_by_transposes)
